import numpy as np
import ml_dtypes


def mxq(x, axis, fmt="e4m3"):
    dtype, down = {"e4m3": (ml_dtypes.float8_e4m3fn, 7), "e5m2": (ml_dtypes.float8_e5m2, 14)}[fmt]
    v = np.moveaxis(np.asarray(x, np.float32).astype(ml_dtypes.bfloat16).astype(np.float64), axis, -1)
    blocks = v.reshape(v.shape[:-1] + (-1, 32))
    amax = np.abs(blocks).max(-1, keepdims=True)
    byte = np.maximum(np.where(amax > 0, np.frexp(amax)[1] - 1 + 127, 0) - down, 1)
    scale = np.exp2(byte - 127.0)
    codes = (blocks / scale).astype(np.float32).astype(dtype).astype(np.float64)
    return np.moveaxis((codes * scale).reshape(v.shape), -1, axis)


WIDE = False


def mx_kscale(k):
    if not WIDE:
        return np.ones(k)
    levels = np.array([10, -10, 5, -5, 0])
    if k % 512:
        return np.exp2(np.random.permutation(np.resize(levels, k // 32))).repeat(32)
    a = np.empty((k // 512, 16))
    for p in range(k // 512):
        a[p, :8] = np.random.permutation(np.resize(levels, 8))
        for g in range(8):
            far = levels[np.abs(levels - a[p, g]) >= 10]
            a[p, g + 8] = far[np.random.randint(len(far))]
    return np.exp2(a.ravel()).repeat(32)


BF16 = ml_dtypes.bfloat16


def bf(x):
    return np.asarray(x, np.float32).astype(BF16)


def f64(x):
    return np.asarray(x).astype(np.float64)


E2M1 = np.array([0.0, 0.5, 1.0, 1.5, 2.0, 3.0, 4.0, 6.0, -0.0, -0.5, -1.0, -1.5, -2.0, -3.0, -4.0, -6.0])


def pack_weight(w, fmt):
    k, n = w.shape
    w = f64(bf(w)).reshape(k // 32, 32, n)
    amax = np.abs(w).max(1)
    if fmt == "e4m3":
        byte = np.frexp(amax)[1] - 1 + 127 - 7
    else:
        mant, ex = np.frexp(amax / 6.0)
        byte = np.where(mant > 0.5, ex, ex - 1) + 127
    byte = np.clip(np.where(amax > 0, byte, 1), 1, 254)
    scaled = (w * np.exp2(127.0 - byte)[:, None, :]).reshape(k, n).astype(np.float32)
    by_word = np.ascontiguousarray(scaled.reshape(k // 512, 128, 4, n).transpose(0, 1, 3, 2))
    if fmt == "e4m3":
        words = by_word.astype(ml_dtypes.float8_e4m3fn).view(np.uint8)
    else:
        c = by_word.astype(ml_dtypes.float4_e2m1fn).view(np.uint8) & 0xF
        words = c[..., 0::2] | (c[..., 1::2] << 4)
    return np.ascontiguousarray(words), np.ascontiguousarray(byte.astype(np.uint8).reshape(k // 512, 16, n))


def unpack_weight(words, scales, fmt):
    g, p, n, _ = words.shape
    if fmt == "e4m3":
        vals = np.ascontiguousarray(words).view(ml_dtypes.float8_e4m3fn).astype(np.float64)
    else:
        nib = np.empty((g, p, n, 4), np.uint8)
        nib[..., 0::2] = words & 0xF
        nib[..., 1::2] = words >> 4
        vals = E2M1[nib]
    vals = vals * np.repeat(np.exp2(scales.astype(np.float64) - 127.0), 8, axis=1)[..., None]
    return vals.transpose(0, 1, 3, 2).reshape(g * 512, n)
def pack4(w):
    words, scales = pack_weight(w, "e2m1")
    return words.reshape(words.shape[0], 128, -1), scales


def unpack4(words, scales):
    return unpack_weight(words.reshape(words.shape[0], 128, -1, 2), scales, "e2m1")


def planes(Y):
    n, m = Y.shape
    b = f64(bf(Y)).reshape(n // 32, 32, m)
    amax = np.abs(b).max(1)
    byte = np.clip(np.where(amax > 0, np.frexp(amax)[1] - 1 + 127 - 7, 1), 1, 254)
    codes = (b * np.exp2(127.0 - byte)[:, None, :]).reshape(n, m).astype(np.float32).astype(ml_dtypes.float8_e4m3fn).view(np.uint8)
    words = codes.reshape(n // 512, 128, 4, m).transpose(0, 1, 3, 2)
    return np.ascontiguousarray(words), np.ascontiguousarray(byte.astype(np.uint8).reshape(n // 512, 16, m))


F, U, P, C = 512, 2, 1024, 1024

def setup_inputs():
    rn = np.random.randn
    s, t, v = mx_kscale(P), mx_kscale(U * P), mx_kscale(C)
    spread = np.exp(0.8 * rn(U * P))
    x = bf(rn(F, U, P) * s)
    d = 0.35 * rn(P, P) / np.sqrt(P) * s[None, :] / s[:, None]
    d_words, d_scales = pack4(d)
    h = bf((1 + 0.1 * rn(U, P)) * t.reshape(U, P) / s)
    wj = bf(0.35 * rn(U * P, C) / np.sqrt(U * P) / t[:, None])
    dt = bf(rn(F, C))
    damp = bf(np.exp(0.3 * rn(C)) * v)
    wg = bf(0.35 * rn(C, U * P) / np.sqrt(C) / v[:, None] * spread)
    unit = bf(((1 + 0.1 * rn(U * P)) * spread / t).reshape(U, P))
    return dict(x=x, d_words=d_words, d_scales=d_scales, h=h, wj=wj, dt=dt, damp=damp, wg=wg, unit=unit)

def reference(x, d_words, d_scales, h, wj, dt, damp, wg, unit):
    x = f64(x)
    off = mxq(x.reshape(F * U, P), 1, "e4m3") @ unpack4(d_words, d_scales)
    wbar = (x + off.reshape(F, U, P)) * f64(h)
    res = mxq(wbar.reshape(F, U * P), 1, "e4m3") @ mxq(f64(wj), 0, "e4m3")
    r = (f64(dt) + res) * f64(damp)
    cor = mxq(r, 1, "e4m3") @ mxq(f64(wg), 0, "e4m3")
    y = wbar * f64(unit) - cor.reshape(F, U, P)
    Y = y.reshape(F * U, P).T
    words, scales = planes(Y)
    return y, words, scales

@@ -1,0 +1,379 @@
+from contextlib import ExitStack
+
+import concourse.mybir as mybir
+from concourse.masks import make_identity
+
+F, U, PIX, C = 512, 2, 1024, 1024
+FLOPS = 2 * (F * U) * PIX * PIX + 2 * F * (U * PIX) * C + 2 * F * C * (U * PIX)
+
+F32 = mybir.dt.float32
+BF16 = mybir.dt.bfloat16
+I32 = mybir.dt.int32
+U32 = mybir.dt.uint32
+U8 = mybir.dt.uint8
+FP8X4 = mybir.dt.float8_e4m3fn_x4
+FP4X4 = mybir.dt.float4_e2m1fn_x4
+ADD = mybir.AluOpType.add
+MULT = mybir.AluOpType.mult
+SUB = mybir.AluOpType.subtract
+
+P = 128
+PACK = 4
+KP = P * PACK
+HALF = F // 2
+RAW_BUFS = 10
+GROUPED_BUFS = 6
+STAGE_BUFS = 5
+
+
+def tile_flow_average_residual_update_k1_kernel(
+    tc, x, d_words, d_scales, h, wj, dt, damp, wg, unit, out_0, out_1, out_2
+):
+    nc = tc.nc
+    with ExitStack() as ctx:
+        keep = ctx.enter_context(tc.tile_pool(name="keep", bufs=1))
+        ring = ctx.enter_context(tc.tile_pool(name="ring", bufs=1))
+        psum = ctx.enter_context(tc.psum_pool(name="psum", bufs=8))
+        ctx.enter_context(tc.manual_schedule())
+
+        def kept(shape, dtype, name):
+            return keep.tile(shape, dtype, name=name, align_bytes=64)
+
+        def new_bank(shape):
+            return psum.tile(shape, F32, name="bank")
+
+        def new_stage():
+            return ring.tile([P, KP * PACK], BF16, name="stage", bufs=STAGE_BUFS, align_bytes=64)
+
+        def new_grouped(shape, dtype):
+            return ring.tile(shape, dtype, name="grouped", bufs=GROUPED_BUFS, align_bytes=64)
+
+        def frame_rows(src, half):
+            return src[HALF * half : HALF * (half + 1), :].rearrange("(a p) n -> p a n", p=P)
+
+        def weight_rows(w, k, col):
+            return w[KP * k : KP * (k + 1), col : col + KP].rearrange("(p j) c -> p j c", j=PACK)
+
+        waiting = []
+        for i in range(U):
+            waiting.extend([(("x", i, half), frame_rows(x[:, i, :], half)) for half in range(2)])
+            waiting.extend([(("wj", i, g), weight_rows(wj, i, KP * g)) for g in range(2)])
+        waiting.extend([(("wj", 2, g), weight_rows(wj, 2, KP * g)) for g in range(2)])
+        waiting.extend([(("dt", 0, half), frame_rows(dt, half)) for half in range(2)])
+        waiting.extend([(("wj", 3, g), weight_rows(wj, 3, KP * g)) for g in range(2)])
+        for g in range(2):
+            for i in range(U):
+                waiting.extend(
+                    [(("wg", k, 2 * i + g), weight_rows(wg, k, PIX * i + KP * g)) for k in range(2)]
+                )
+        raw = {}
+
+        def load_next(count):
+            for key, src in waiting[len(raw) : len(raw) + count]:
+                raw[key] = ring.tile(list(src.shape), BF16, name="raw", bufs=RAW_BUFS, align_bytes=64)
+                nc.sync.dma_start(out=raw[key][:], in_=src)
+
+        ident = kept([P, P], F32, "ident")
+        make_identity(nc, ident[:])
+
+        d_raw = kept([P, 2, 2 * PIX], U8, "d_raw")
+        d_raw_scales = kept([P, 2, PIX], U8, "d_raw_scales")
+        nc.vector.memset(d_raw_scales[:].bitcast(I32), 0)
+        nc.sync.dma_start(out=d_raw[:].bitcast(I32), in_=d_words.rearrange("k p n -> p k n").bitcast(I32))
+        for q in range(4):
+            nc.sync.dma_start(
+                out=d_raw_scales[32 * q : 32 * q + 4, :, :].bitcast(I32),
+                in_=d_scales[:, 4 * q : 4 * q + 4, :].rearrange("k r n -> r k n").bitcast(I32),
+            )
+        load_next(2)
+        h_col = kept([P, 4, PACK], BF16, "h_col")
+        unit_col = kept([P, 4, PACK], BF16, "unit_col")
+        damp_col = kept([P, 2, PACK], BF16, "damp_col")
+        hu_col = kept([P, 4, PACK], F32, "hu_col")
+        nc.sync.dma_start(out=h_col[:], in_=h.rearrange("i (g p t) -> p (i g) t", p=P, t=PACK))
+        load_next(4)
+        nc.sync.dma_start(out=unit_col[:], in_=unit.rearrange("i (g p t) -> p (i g) t", p=P, t=PACK))
+        nc.sync.dma_start(out=damp_col[:], in_=damp.rearrange("(g p t) -> p g t", p=P, t=PACK))
+        load_next(RAW_BUFS - 6)
+
+        d_codes, d_planes = {}, {}
+
+        def order_d_codes(g):
+            d_codes[g] = kept([P, 2, PACK, 2 * P], U8, "d_codes%d" % g)
+            for k in range(2):
+                nc.vector.tensor_copy(
+                    out=d_codes[g][:, k, :, :].rearrange("p t (mm m b) -> p mm t m b", m=8, b=2),
+                    in_=d_raw[:, k, 2 * KP * g : 2 * KP * (g + 1)].rearrange(
+                        "p (mm m t b) -> p mm t m b", m=8, t=PACK, b=2
+                    ),
+                )
+
+        def order_d_scales(g):
+            d_planes[g] = kept([P, 2, PACK, P], U8, "d_planes%d" % g)
+            nc.vector.tensor_copy(
+                out=d_planes[g][:].rearrange("p k t (mm m) -> p k mm t m", m=16),
+                in_=d_raw_scales[:, :, KP * g : KP * (g + 1)].rearrange(
+                    "p k (mm m t) -> p k mm t m", m=16, t=PACK
+                ),
+            )
+
+        grouped = {}
+
+        def turn(name, i, half):
+            words = raw[name, i, half][:].bitcast(F32)
+            for k in range(2):
+                if half == 0:
+                    grouped[name, i, k] = new_grouped([P, F * PACK], BF16)
+                bank = new_bank([P, 2, HALF])
+                for a in range(2):
+                    for u in range(2):
+                        nc.tensor.transpose(
+                            bank[:, u, P * a : P * (a + 1)],
+                            words[:, a, 2 * P * k + u : 2 * P * (k + 1) : 2],
+                            ident[:],
+                        )
+                dst = grouped[name, i, k][:].bitcast(F32)[:, 2 * HALF * half : 2 * HALF * (half + 1)]
+                nc.scalar.copy(
+                    out=dst.rearrange("p (r u) -> p r u", u=2), in_=bank[:].rearrange("p u r -> p r u")
+                )
+            load_next(1)
+
+        codes, planes = {}, {}
+
+        def quantize(key, src):
+            label = "_".join([str(part) for part in key])
+            codes[key] = kept([P, KP], U32, "codes_" + label)
+            planes[key] = kept([P, KP], U8, "planes_" + label)
+            nc.vector.quantize_mx(out=codes[key][:].bitcast(FP8X4), scales=planes[key][:], in_=src[:])
+
+        staged = {}
+
+        def lay_weight(key, engine_copy):
+            staged[key] = new_stage()
+            engine_copy(
+                out=staged[key][:].rearrange("p (t mm m j) -> p mm t m j", t=PACK, m=2, j=PACK),
+                in_=raw[key][:].rearrange("p j (mm m t) -> p mm t m j", m=2, t=PACK),
+            )
+            load_next(1)
+
+        def quantize_staged(key):
+            quantize(key, staged[key])
+
+        banks = {}
+
+        def passes(stage, unit_key, ks, depth):
+            for t in range(PACK):
+                if ks[0] == 0:
+                    banks[stage, unit_key, t] = new_bank([P, F])
+                for k in ks:
+                    if stage == 1:
+                        i, g = divmod(unit_key, 2)
+                        lhs = d_codes[g][:, k, t, :].bitcast(FP4X4)
+                        lhs_scale = d_planes[g][:, k, t, :]
+                        moving = ("x", i, k)
+                    else:
+                        wkey = ("wj" if stage == 2 else "wg", k, unit_key)
+                        lhs = codes[wkey][:, P * t : P * (t + 1)].bitcast(FP8X4)
+                        lhs_scale = planes[wkey][:, P * t : P * (t + 1)]
+                        moving = ("wbar" if stage == 2 else "r", k)
+                    nc.tensor.matmul_mx(
+                        out=banks[stage, unit_key, t][:],
+                        lhsT=lhs,
+                        lhsT_scale=lhs_scale,
+                        rhs=codes[moving][:].bitcast(FP8X4),
+                        rhs_scale=planes[moving][:],
+                        start=(k == 0),
+                        stop=(k == depth - 1),
+                    )
+
+        flow = [kept([P, U, PACK, F], F32, "flow%d" % g) for g in range(2)]
+        resid = [kept([P, PACK, F], F32, "resid%d" % g) for g in range(2)]
+
+        def add_input(stage, unit_key, sums, addend):
+            columns = addend[:].rearrange("p (f t) -> p f t", t=PACK)
+            for t in range(PACK):
+                nc.vector.tensor_tensor(
+                    out=sums[:, t, :], in0=banks[stage, unit_key, t][:], in1=columns[:, :, t], op=ADD
+                )
+
+        def scale_round(key, sums, factor):
+            staged[key] = new_stage()
+            nc.vector.tensor_tensor(
+                out=staged[key][:].rearrange("p (c e t) -> p c t e", e=2, t=PACK),
+                in0=sums.rearrange("p t (c e) -> p c t e", e=2),
+                in1=factor.unsqueeze(1).unsqueeze(3).to_broadcast([P, F // 2, PACK, 2]),
+                op=MULT,
+            )
+
+        def add_x(kk):
+            i, g = divmod(kk, 2)
+            add_input(1, kk, flow[g][:, i, :, :], grouped["x", i, g])
+
+        def scale_wbar(kk):
+            i, g = divmod(kk, 2)
+            scale_round(("wbar", kk), flow[g][:, i, :, :], h_col[:, kk, :])
+
+        def add_dt(g):
+            add_input(2, g, resid[g][:], grouped["dt", 0, g])
+
+        def scale_r(g):
+            scale_round(("r", g), resid[g][:], damp_col[:, g, :])
+
+        def finish_y(kk):
+            i, g = divmod(kk, 2)
+            for t in range(PACK):
+                nc.vector.scalar_tensor_tensor(
+                    out=flow[g][:, i, t, :],
+                    in0=flow[g][:, i, t, :],
+                    scalar=hu_col[:, kk, t : t + 1],
+                    in1=banks[3, kk, t][:],
+                    op0=MULT,
+                    op1=SUB,
+                )
+
+        def store_y(kk, half):
+            i, g = divmod(kk, 2)
+            rows = new_grouped([P, 2, KP], F32)
+            for a in range(2):
+                bank = new_bank([P, PACK, P])
+                f0 = HALF * half + P * a
+                for t in range(PACK):
+                    nc.tensor.transpose(bank[:, t, :], flow[g][:, i, t, f0 : f0 + P], ident[:])
+                nc.scalar.copy(
+                    out=rows[:, a, :].rearrange("p (m t) -> p m t", t=PACK),
+                    in_=bank[:].rearrange("p t m -> p m t"),
+                )
+            nc.sync.dma_start(out=frame_rows(out_0[:, i, KP * g : KP * (g + 1)], half), in_=rows[:])
+
+        def round_y(g, half, engine_copy):
+            staged["y", g, half] = new_stage()
+            engine_copy(
+                out=staged["y", g, half][:].rearrange("p (c e i t) -> p c i t e", e=2, i=U, t=PACK),
+                in_=flow[g][:, :, :, HALF * half : HALF * (half + 1)].rearrange(
+                    "p i t (c e) -> p c i t e", e=2
+                ),
+            )
+
+        y_planes = [kept([P, F * U], U8, "y_planes%d" % g) for g in range(2)]
+
+        def quantize_y(g, half):
+            y_codes = kept([P, KP], U32, "y_codes%d_%d" % (g, half))
+            cols = slice(KP * half, KP * (half + 1))
+            nc.vector.quantize_mx(
+                out=y_codes[:].bitcast(FP8X4), scales=y_planes[g][:, cols], in_=staged["y", g, half][:]
+            )
+            nc.sync.dma_start(
+                out=out_1[g].rearrange("p m t -> p (m t)").bitcast(I32)[:, cols], in_=y_codes[:].bitcast(I32)
+            )
+
+        def store_y_planes(g):
+            for q in range(4):
+                nc.sync.dma_start(
+                    out=out_2[g, 4 * q : 4 * q + 4, :].bitcast(I32),
+                    in_=y_planes[g][32 * q : 32 * q + 4, :].bitcast(I32),
+                )
+
+        on_scalar = nc.scalar.copy
+        on_vector = nc.vector.tensor_copy
+
+        order_d_codes(0)
+        turn("x", 0, 0)
+        order_d_scales(0)
+        turn("x", 0, 1)
+        order_d_codes(1)
+        quantize(("x", 0, 0), grouped["x", 0, 0])
+        quantize(("x", 0, 1), grouped["x", 0, 1])
+        passes(1, 0, [0, 1], 2)
+        order_d_scales(1)
+        passes(1, 1, [0, 1], 2)
+        lay_weight(("wj", 0, 0), on_scalar)
+        lay_weight(("wj", 0, 1), on_scalar)
+        add_x(0)
+        nc.vector.tensor_tensor(out=hu_col[:], in0=h_col[:], in1=unit_col[:], op=MULT)
+        turn("x", 1, 0)
+        turn("x", 1, 1)
+        scale_wbar(0)
+        quantize_staged(("wj", 0, 0))
+        add_x(1)
+        quantize_staged(("wbar", 0))
+        quantize_staged(("wj", 0, 1))
+        lay_weight(("wj", 1, 0), on_scalar)
+        lay_weight(("wj", 1, 1), on_scalar)
+        quantize(("x", 1, 0), grouped["x", 1, 0])
+        quantize(("x", 1, 1), grouped["x", 1, 1])
+        passes(1, 2, [0, 1], 2)
+        passes(1, 3, [0, 1], 2)
+        scale_wbar(1)
+        quantize_staged(("wj", 1, 0))
+        quantize_staged(("wbar", 1))
+        add_x(2)
+        lay_weight(("wj", 2, 0), on_scalar)
+        lay_weight(("wj", 2, 1), on_scalar)
+        quantize_staged(("wj", 1, 1))
+        turn("dt", 0, 0)
+        turn("dt", 0, 1)
+        scale_wbar(2)
+        quantize_staged(("wj", 2, 0))
+        quantize_staged(("wbar", 2))
+        lay_weight(("wj", 3, 0), on_scalar)
+        lay_weight(("wj", 3, 1), on_scalar)
+        add_x(3)
+        quantize_staged(("wj", 2, 1))
+        passes(2, 0, [0, 1, 2], 4)
+        passes(2, 1, [0, 1, 2], 4)
+        scale_wbar(3)
+        quantize_staged(("wj", 3, 0))
+        quantize_staged(("wbar", 3))
+        quantize_staged(("wj", 3, 1))
+        passes(2, 0, [3], 4)
+        passes(2, 1, [3], 4)
+        lay_weight(("wg", 0, 0), on_scalar)
+        lay_weight(("wg", 1, 0), on_scalar)
+        lay_weight(("wg", 0, 2), on_vector)
+        add_dt(0)
+        quantize_staged(("wg", 0, 2))
+        scale_r(0)
+        quantize_staged(("wg", 0, 0))
+        lay_weight(("wg", 1, 2), on_scalar)
+        lay_weight(("wg", 0, 1), on_scalar)
+        quantize_staged(("r", 0))
+        add_dt(1)
+        quantize_staged(("wg", 1, 0))
+        passes(3, 0, [0], 2)
+        passes(3, 2, [0], 2)
+        scale_r(1)
+        quantize_staged(("wg", 1, 2))
+        quantize_staged(("r", 1))
+        lay_weight(("wg", 1, 1), on_scalar)
+        lay_weight(("wg", 0, 3), on_scalar)
+        lay_weight(("wg", 1, 3), on_scalar)
+        passes(3, 0, [1], 2)
+        passes(3, 2, [1], 2)
+        quantize_staged(("wg", 0, 1))
+        quantize_staged(("wg", 1, 1))
+        finish_y(0)
+        passes(3, 1, [0, 1], 2)
+        quantize_staged(("wg", 0, 3))
+        finish_y(2)
+        store_y(0, 0)
+        store_y(0, 1)
+        quantize_staged(("wg", 1, 3))
+        round_y(0, 0, on_scalar)
+        round_y(0, 1, on_vector)
+        finish_y(1)
+        passes(3, 3, [0, 1], 2)
+        store_y(2, 0)
+        store_y(2, 1)
+        quantize_y(0, 1)
+        quantize_y(0, 0)
+        store_y_planes(0)
+        finish_y(3)
+        store_y(1, 0)
+        store_y(1, 1)
+        round_y(1, 0, on_vector)
+        round_y(1, 1, on_vector)
+        store_y(3, 0)
+        quantize_y(1, 0)
+        store_y(3, 1)
+        quantize_y(1, 1)
+        store_y_planes(1)

@@ -16,6 +16,7 @@ FP4X4 = mybir.dt.float4_e2m1fn_x4
 ADD = mybir.AluOpType.add
 MULT = mybir.AluOpType.mult
 SUB = mybir.AluOpType.subtract
+COPY = mybir.ActivationFunctionType.Copy
 
 P = 128
 PACK = 4
@@ -23,7 +24,7 @@ KP = P * PACK
 HALF = F // 2
 RAW_BUFS = 10
 GROUPED_BUFS = 6
-STAGE_BUFS = 5
+STAGE_BUFS = 7
 
 
 def tile_flow_average_residual_update_k1_kernel(
@@ -33,14 +34,14 @@ def tile_flow_average_residual_update_k1_kernel(
     with ExitStack() as ctx:
         keep = ctx.enter_context(tc.tile_pool(name="keep", bufs=1))
         ring = ctx.enter_context(tc.tile_pool(name="ring", bufs=1))
-        psum = ctx.enter_context(tc.psum_pool(name="psum", bufs=8))
+        psum = ctx.enter_context(tc.psum_pool(name="psum", bufs=1))
         ctx.enter_context(tc.manual_schedule())
 
         def kept(shape, dtype, name):
             return keep.tile(shape, dtype, name=name, align_bytes=64)
 
-        def new_bank(shape):
-            return psum.tile(shape, F32, name="bank")
+        def new_bank(shape, number, dtype=F32):
+            return psum.tile(shape, dtype, name="bank%d" % number)
 
         def new_stage():
             return ring.tile([P, KP * PACK], BF16, name="stage", bufs=STAGE_BUFS, align_bytes=64)
@@ -54,18 +55,23 @@ def tile_flow_average_residual_update_k1_kernel(
         def weight_rows(w, k, col):
             return w[KP * k : KP * (k + 1), col : col + KP].rearrange("(p j) c -> p j c", j=PACK)
 
-        waiting = []
-        for i in range(U):
-            waiting.extend([(("x", i, half), frame_rows(x[:, i, :], half)) for half in range(2)])
-            waiting.extend([(("wj", i, g), weight_rows(wj, i, KP * g)) for g in range(2)])
-        waiting.extend([(("wj", 2, g), weight_rows(wj, 2, KP * g)) for g in range(2)])
-        waiting.extend([(("dt", 0, half), frame_rows(dt, half)) for half in range(2)])
-        waiting.extend([(("wj", 3, g), weight_rows(wj, 3, KP * g)) for g in range(2)])
-        for g in range(2):
-            for i in range(U):
-                waiting.extend(
-                    [(("wg", k, 2 * i + g), weight_rows(wg, k, PIX * i + KP * g)) for k in range(2)]
-                )
+        def source(key):
+            name, a, b = key
+            if name == "x":
+                return frame_rows(x[:, a, :], b)
+            if name == "dt":
+                return frame_rows(dt, b)
+            if name == "wj":
+                return weight_rows(wj, a, KP * b)
+            return weight_rows(wg, a, PIX * (b // 2) + KP * (b % 2))
+
+        load_order = [
+            ("x", 0, 0), ("x", 0, 1), ("wj", 0, 0), ("wj", 1, 0), ("wj", 1, 1), ("wj", 0, 1),
+            ("x", 1, 0), ("x", 1, 1), ("wg", 0, 0), ("dt", 0, 0), ("dt", 0, 1), ("wj", 2, 0), ("wj", 2, 1),
+            ("wg", 1, 0), ("wj", 3, 0), ("wg", 0, 2), ("wj", 3, 1), ("wg", 1, 2), ("wg", 0, 1), ("wg", 1, 1),
+            ("wg", 1, 3), ("wg", 0, 3),
+        ]
+        waiting = [(key, source(key)) for key in load_order]
         raw = {}
 
         def load_next(count):
@@ -75,35 +81,45 @@ def tile_flow_average_residual_update_k1_kernel(
 
         ident = kept([P, P], F32, "ident")
         make_identity(nc, ident[:])
+        ident16 = kept([P, P], BF16, "ident16")
+        make_identity(nc, ident16[:])
 
-        d_raw = kept([P, 2, 2 * PIX], U8, "d_raw")
+        def new_side(shape, dtype):
+            return ring.tile(shape, dtype, name="side", bufs=1, align_bytes=64)
+
+        d_raw = [kept([P, 2, 2 * KP], U8, "d_raw0"), new_side([P, 2, 2 * KP], U8)]
         d_raw_scales = kept([P, 2, PIX], U8, "d_raw_scales")
         nc.vector.memset(d_raw_scales[:].bitcast(I32), 0)
-        nc.sync.dma_start(out=d_raw[:].bitcast(I32), in_=d_words.rearrange("k p n -> p k n").bitcast(I32))
+        factor_rows = kept([P, KP], BF16, "factor_rows")
+        nc.vector.memset(factor_rows[:], 0.0)
+
+        def load_d(g):
+            src = d_words[:, :, 2 * KP * g : 2 * KP * (g + 1)].rearrange("k p n -> p k n")
+            nc.sync.dma_start(out=d_raw[g][:].bitcast(I32), in_=src.bitcast(I32))
+
+        load_d(0)
         for q in range(4):
             nc.sync.dma_start(
                 out=d_raw_scales[32 * q : 32 * q + 4, :, :].bitcast(I32),
                 in_=d_scales[:, 4 * q : 4 * q + 4, :].rearrange("k r n -> r k n").bitcast(I32),
             )
         load_next(2)
-        h_col = kept([P, 4, PACK], BF16, "h_col")
-        unit_col = kept([P, 4, PACK], BF16, "unit_col")
-        damp_col = kept([P, 2, PACK], BF16, "damp_col")
-        hu_col = kept([P, 4, PACK], F32, "hu_col")
-        nc.sync.dma_start(out=h_col[:], in_=h.rearrange("i (g p t) -> p (i g) t", p=P, t=PACK))
-        load_next(4)
-        nc.sync.dma_start(out=unit_col[:], in_=unit.rearrange("i (g p t) -> p (i g) t", p=P, t=PACK))
-        nc.sync.dma_start(out=damp_col[:], in_=damp.rearrange("(g p t) -> p g t", p=P, t=PACK))
-        load_next(RAW_BUFS - 6)
+        load_d(1)
+        nc.sync.dma_start(out=factor_rows[0:4, :], in_=h.rearrange("i (g n) -> (i g) n", g=2))
+        load_next(1)
+        nc.sync.dma_start(out=factor_rows[4:8, :], in_=unit.rearrange("i (g n) -> (i g) n", g=2))
+        nc.sync.dma_start(out=factor_rows[8:10, :], in_=damp.rearrange("(g n) -> g n", g=2))
+        load_next(RAW_BUFS - 3)
 
         d_codes, d_planes = {}, {}
 
-        def order_d_codes(g):
-            d_codes[g] = kept([P, 2, PACK, 2 * P], U8, "d_codes%d" % g)
-            for k in range(2):
+        def order_d_codes(g, ks):
+            if ks[0] == 0:
+                d_codes[g] = kept([P, 2, PACK, 2 * P], U8, "d_codes%d" % g)
+            for k in ks:
                 nc.vector.tensor_copy(
                     out=d_codes[g][:, k, :, :].rearrange("p t (mm m b) -> p mm t m b", m=8, b=2),
-                    in_=d_raw[:, k, 2 * KP * g : 2 * KP * (g + 1)].rearrange(
+                    in_=d_raw[g][:, k, :].rearrange(
                         "p (mm m t b) -> p mm t m b", m=8, t=PACK, b=2
                     ),
                 )
@@ -119,12 +135,12 @@ def tile_flow_average_residual_update_k1_kernel(
 
         grouped = {}
 
-        def turn(name, i, half):
+        def turn(name, i, half, numbers):
             words = raw[name, i, half][:].bitcast(F32)
             for k in range(2):
                 if half == 0:
                     grouped[name, i, k] = new_grouped([P, F * PACK], BF16)
-                bank = new_bank([P, 2, HALF])
+                bank = new_bank([P, 2, HALF], numbers[k])
                 for a in range(2):
                     for u in range(2):
                         nc.tensor.transpose(
@@ -137,6 +153,35 @@ def tile_flow_average_residual_update_k1_kernel(
                     out=dst.rearrange("p (r u) -> p r u", u=2), in_=bank[:].rearrange("p u r -> p r u")
                 )
             load_next(1)
+
+        factors = new_bank([P, PACK, P], 7, BF16)
+        unit_damp = kept([P, PACK, 6], F32, "unit_damp")
+        hu_col = kept([P, PACK, 4], F32, "hu_col")
+
+        def turn_factors():
+            for t in range(PACK):
+                nc.tensor.transpose(factors[:, t, :], factor_rows[:, t:KP:PACK], ident16[:])
+            nc.scalar.copy(out=unit_damp[:], in_=factors[:, :, 4:10])
+
+        dt_damped = [kept([P, PACK, F], F32, "dt_damped%d" % g) for g in range(2)]
+
+        def turn_dt(g):
+            for u in range(2):
+                bank = new_bank([P, F], 2 + u)
+                for a in range(4):
+                    words = raw["dt", 0, a // 2][:].bitcast(F32)
+                    nc.tensor.transpose(
+                        bank[:, P * a : P * (a + 1)],
+                        words[:, a % 2, 2 * P * g + u : 2 * P * (g + 1) : 2],
+                        ident[:],
+                    )
+                pairs = bank[:].bitcast(BF16).rearrange("p (f e) -> p f e", e=2)
+                for e in range(2):
+                    t = 2 * u + e
+                    nc.scalar.activation(
+                        out=dt_damped[g][:, t, :], in_=pairs[:, :, e], func=COPY,
+                        scale=unit_damp[:, t, 4 + g : 5 + g],
+                    )
 
         codes, planes = {}, {}
 
@@ -159,12 +204,45 @@ def tile_flow_average_residual_update_k1_kernel(
         def quantize_staged(key):
             quantize(key, staged[key])
 
-        banks = {}
+        side = {}
 
-        def passes(stage, unit_key, ks, depth):
-            for t in range(PACK):
+        def lay_on_gpsimd(pieces):
+            tile = new_side([P, 5 * 2 * KP], BF16)
+            col = 0
+            for key, t0, t1 in pieces:
+                width = (t1 - t0) * KP
+                side[key, t0] = tile[:, col : col + width]
+                nc.gpsimd.tensor_scalar(
+                    out=side[key, t0].rearrange("p (t m j) -> p t m j", m=P, j=PACK),
+                    in0=raw[key][:].rearrange("p j (m t) -> p t m j", t=PACK)[:, t0:t1, :, :],
+                    scalar1=1.0, scalar2=0.0, op0=MULT, op1=ADD,
+                )
+                col = col + width
+                if t1 == PACK:
+                    load_next(1)
+
+        def quantize_side(pieces):
+            for key, t0, t1 in pieces:
+                if t0 == 0:
+                    label = "_".join([str(part) for part in key])
+                    codes[key] = kept([P, KP], U32, "codes_" + label)
+                    planes[key] = kept([P, KP], U8, "planes_" + label)
+                cols = slice(P * t0, P * t1)
+                nc.vector.quantize_mx(
+                    out=codes[key][:, cols].bitcast(FP8X4), scales=planes[key][:, cols], in_=side[key, t0]
+                )
+
+        banks = {}
+        low, high = [0, 1, 2, 3], [4, 5, 6, 7]
+        bank_of = {
+            (1, 0): [4, 5, 6, 0], (1, 1): [1, 2, 3, 4], (1, 2): [4, 5, 6, 0], (1, 3): [1, 2, 3, 4],
+            (2, 0): low, (2, 1): high, (3, 0): low, (3, 2): high, (3, 1): high, (3, 3): high,
+        }
+
+        def passes(stage, unit_key, ks, depth, slots=range(PACK)):
+            for t in slots:
                 if ks[0] == 0:
-                    banks[stage, unit_key, t] = new_bank([P, F])
+                    banks[stage, unit_key, t] = new_bank([P, F], bank_of[stage, unit_key][t])
                 for k in ks:
                     if stage == 1:
                         i, g = divmod(unit_key, 2)
@@ -187,7 +265,6 @@ def tile_flow_average_residual_update_k1_kernel(
                     )
 
         flow = [kept([P, U, PACK, F], F32, "flow%d" % g) for g in range(2)]
-        resid = [kept([P, PACK, F], F32, "resid%d" % g) for g in range(2)]
 
         def add_input(stage, unit_key, sums, addend):
             columns = addend[:].rearrange("p (f t) -> p f t", t=PACK)
@@ -211,21 +288,36 @@ def tile_flow_average_residual_update_k1_kernel(
 
         def scale_wbar(kk):
             i, g = divmod(kk, 2)
-            scale_round(("wbar", kk), flow[g][:, i, :, :], h_col[:, kk, :])
+            scale_round(("wbar", kk), flow[g][:, i, :, :], factors[:, :, kk])
 
-        def add_dt(g):
-            add_input(2, g, resid[g][:], grouped["dt", 0, g])
+        resid = {}
 
-        def scale_r(g):
-            scale_round(("r", g), resid[g][:], damp_col[:, g, :])
-
-        def finish_y(kk):
-            i, g = divmod(kk, 2)
+        def finish_r(g):
+            resid[g] = new_stage()
             for t in range(PACK):
+                nc.vector.scalar_tensor_tensor(
+                    out=resid[g][:, F * t : F * (t + 1)],
+                    in0=banks[2, g, t][:],
+                    scalar=unit_damp[:, t, 4 + g : 5 + g],
+                    in1=dt_damped[g][:, t, :],
+                    op0=MULT,
+                    op1=ADD,
+                )
+
+        def lay_r(g, engine_copy):
+            staged["r", g] = new_stage()
+            engine_copy(
+                out=staged["r", g][:].rearrange("p (c e t) -> p c t e", e=4, t=PACK),
+                in_=resid[g][:].rearrange("p (t c e) -> p c t e", t=PACK, e=4),
+            )
+
+        def finish_y(kk, slots=range(PACK)):
+            i, g = divmod(kk, 2)
+            for t in slots:
                 nc.vector.scalar_tensor_tensor(
                     out=flow[g][:, i, t, :],
                     in0=flow[g][:, i, t, :],
-                    scalar=hu_col[:, kk, t : t + 1],
+                    scalar=hu_col[:, t, kk : kk + 1],
                     in1=banks[3, kk, t][:],
                     op0=MULT,
                     op1=SUB,
@@ -235,7 +327,7 @@ def tile_flow_average_residual_update_k1_kernel(
             i, g = divmod(kk, 2)
             rows = new_grouped([P, 2, KP], F32)
             for a in range(2):
-                bank = new_bank([P, PACK, P])
+                bank = new_bank([P, PACK, P], 2 * half + a)
                 f0 = HALF * half + P * a
                 for t in range(PACK):
                     nc.tensor.transpose(bank[:, t, :], flow[g][:, i, t, f0 : f0 + P], ident[:])
@@ -245,12 +337,15 @@ def tile_flow_average_residual_update_k1_kernel(
                 )
             nc.sync.dma_start(out=frame_rows(out_0[:, i, KP * g : KP * (g + 1)], half), in_=rows[:])
 
+        def on_gpsimd(out, in_):
+            nc.gpsimd.tensor_scalar(out=out, in0=in_, scalar1=1.0, scalar2=0.0, op0=MULT, op1=ADD)
+
         def round_y(g, half, engine_copy):
-            staged["y", g, half] = new_stage()
+            staged["y", g, half] = new_side([P, KP * PACK], BF16) if g == 0 else new_stage()
             engine_copy(
-                out=staged["y", g, half][:].rearrange("p (c e i t) -> p c i t e", e=2, i=U, t=PACK),
+                out=staged["y", g, half][:].rearrange("p (c e s) -> p c s e", e=2, s=U * PACK),
                 in_=flow[g][:, :, :, HALF * half : HALF * (half + 1)].rearrange(
-                    "p i t (c e) -> p c i t e", e=2
+                    "p i t (c e) -> p c (i t) e", e=2
                 ),
             )
 
@@ -276,104 +371,115 @@ def tile_flow_average_residual_update_k1_kernel(
         on_scalar = nc.scalar.copy
         on_vector = nc.vector.tensor_copy
 
-        order_d_codes(0)
-        turn("x", 0, 0)
+        side_work = [
+            [(("wj", 1, 0), 0, 4), (("wj", 1, 1), 0, 4), (("wg", 0, 0), 0, 2)],
+            [(("wg", 0, 0), 2, 4), (("wg", 1, 0), 0, 4), (("wg", 0, 2), 0, 4)],
+            [(("wg", 1, 3), 0, 4)],
+        ]
+        order_d_codes(0, [0, 1])
+        turn("x", 0, 0, [0, 1])
         order_d_scales(0)
-        turn("x", 0, 1)
-        order_d_codes(1)
+        turn("x", 0, 1, [2, 3])
+        turn_factors()
+        order_d_scales(1)
+        order_d_codes(1, [0])
         quantize(("x", 0, 0), grouped["x", 0, 0])
         quantize(("x", 0, 1), grouped["x", 0, 1])
-        passes(1, 0, [0, 1], 2)
-        order_d_scales(1)
-        passes(1, 1, [0, 1], 2)
+        passes(1, 0, [0], 2)
+        passes(1, 0, [1], 2)
+        order_d_codes(1, [1])
         lay_weight(("wj", 0, 0), on_scalar)
+        lay_on_gpsimd(side_work[0])
         lay_weight(("wj", 0, 1), on_scalar)
+        passes(1, 1, [0, 1], 2, range(3))
         add_x(0)
-        nc.vector.tensor_tensor(out=hu_col[:], in0=h_col[:], in1=unit_col[:], op=MULT)
-        turn("x", 1, 0)
-        turn("x", 1, 1)
-        scale_wbar(0)
-        quantize_staged(("wj", 0, 0))
+        passes(1, 1, [0, 1], 2, [3])
+        turn("x", 1, 0, [5, 6])
         add_x(1)
-        quantize_staged(("wbar", 0))
-        quantize_staged(("wj", 0, 1))
-        lay_weight(("wj", 1, 0), on_scalar)
-        lay_weight(("wj", 1, 1), on_scalar)
+        turn("x", 1, 1, [0, 1])
+        turn_dt(0)
+        turn_dt(1)
+        load_next(2)
+        scale_wbar(0)
+        scale_wbar(1)
+        nc.vector.tensor_tensor(out=hu_col[:], in0=factors[:, :, 0:4], in1=unit_damp[:, :, 0:4], op=MULT)
         quantize(("x", 1, 0), grouped["x", 1, 0])
         quantize(("x", 1, 1), grouped["x", 1, 1])
         passes(1, 2, [0, 1], 2)
-        passes(1, 3, [0, 1], 2)
-        scale_wbar(1)
-        quantize_staged(("wj", 1, 0))
+        passes(1, 3, [0, 1], 2, range(3))
+        quantize_staged(("wj", 0, 0))
+        quantize_staged(("wj", 0, 1))
+        quantize_staged(("wbar", 0))
         quantize_staged(("wbar", 1))
-        add_x(2)
         lay_weight(("wj", 2, 0), on_scalar)
         lay_weight(("wj", 2, 1), on_scalar)
-        quantize_staged(("wj", 1, 1))
-        turn("dt", 0, 0)
-        turn("dt", 0, 1)
-        scale_wbar(2)
-        quantize_staged(("wj", 2, 0))
-        quantize_staged(("wbar", 2))
         lay_weight(("wj", 3, 0), on_scalar)
         lay_weight(("wj", 3, 1), on_scalar)
+        quantize_side(side_work[0])
+        lay_on_gpsimd(side_work[1])
+        add_x(2)
+        passes(1, 3, [0, 1], 2, [3])
         add_x(3)
-        quantize_staged(("wj", 2, 1))
-        passes(2, 0, [0, 1, 2], 4)
-        passes(2, 1, [0, 1, 2], 4)
+        passes(2, 0, [0, 1], 4)
+        passes(2, 1, [0, 1], 4, range(3))
+        scale_wbar(2)
         scale_wbar(3)
-        quantize_staged(("wj", 3, 0))
-        quantize_staged(("wbar", 3))
-        quantize_staged(("wj", 3, 1))
-        passes(2, 0, [3], 4)
-        passes(2, 1, [3], 4)
-        lay_weight(("wg", 0, 0), on_scalar)
-        lay_weight(("wg", 1, 0), on_scalar)
-        lay_weight(("wg", 0, 2), on_vector)
-        add_dt(0)
-        quantize_staged(("wg", 0, 2))
-        scale_r(0)
-        quantize_staged(("wg", 0, 0))
+        passes(2, 1, [0, 1], 4, [3])
+        quantize_staged(("wj", 2, 0))
+        quantize_staged(("wbar", 2))
+        passes(2, 0, [2], 4)
         lay_weight(("wg", 1, 2), on_scalar)
         lay_weight(("wg", 0, 1), on_scalar)
+        quantize_staged(("wj", 3, 0))
+        quantize_staged(("wbar", 3))
+        passes(2, 0, [3], 4)
+        quantize_staged(("wj", 2, 1))
+        quantize_staged(("wj", 3, 1))
+        passes(2, 1, [2, 3], 4)
+        lay_weight(("wg", 1, 1), on_scalar)
+        quantize_side(side_work[1])
+        lay_on_gpsimd(side_work[2])
+        finish_r(0)
+        lay_r(0, on_scalar)
+        finish_r(1)
+        lay_r(1, on_scalar)
+        quantize_staged(("wg", 1, 2))
+        lay_weight(("wg", 0, 3), on_scalar)
+        quantize_staged(("wg", 0, 1))
         quantize_staged(("r", 0))
-        add_dt(1)
-        quantize_staged(("wg", 1, 0))
         passes(3, 0, [0], 2)
         passes(3, 2, [0], 2)
-        scale_r(1)
-        quantize_staged(("wg", 1, 2))
+        quantize_staged(("wg", 1, 1))
         quantize_staged(("r", 1))
-        lay_weight(("wg", 1, 1), on_scalar)
-        lay_weight(("wg", 0, 3), on_scalar)
-        lay_weight(("wg", 1, 3), on_scalar)
         passes(3, 0, [1], 2)
         passes(3, 2, [1], 2)
-        quantize_staged(("wg", 0, 1))
-        quantize_staged(("wg", 1, 1))
+        quantize_side(side_work[2])
         finish_y(0)
-        passes(3, 1, [0, 1], 2)
-        quantize_staged(("wg", 0, 3))
-        finish_y(2)
         store_y(0, 0)
+        finish_y(2)
+        passes(3, 1, [0, 1], 2, [0])
         store_y(0, 1)
-        quantize_staged(("wg", 1, 3))
-        round_y(0, 0, on_scalar)
-        round_y(0, 1, on_vector)
-        finish_y(1)
-        passes(3, 3, [0, 1], 2)
+        passes(3, 1, [0, 1], 2, [1, 2])
         store_y(2, 0)
+        passes(3, 1, [0, 1], 2, [3])
         store_y(2, 1)
-        quantize_y(0, 1)
+        round_y(0, 0, on_vector)
+        quantize_staged(("wg", 0, 3))
         quantize_y(0, 0)
-        store_y_planes(0)
-        finish_y(3)
+        round_y(0, 1, on_gpsimd)
+        finish_y(1)
+        passes(3, 3, [0, 1], 2, [0, 1, 2])
         store_y(1, 0)
+        passes(3, 3, [0, 1], 2, [3])
         store_y(1, 1)
+        finish_y(3, [0, 1])
+        quantize_y(0, 1)
+        store_y_planes(0)
+        finish_y(3, [2, 3])
         round_y(1, 0, on_vector)
-        round_y(1, 1, on_vector)
         store_y(3, 0)
-        quantize_y(1, 0)
+        round_y(1, 1, on_vector)
         store_y(3, 1)
+        quantize_y(1, 0)
         quantize_y(1, 1)
         store_y_planes(1)

@@ -23,8 +23,8 @@ PACK = 4
 KP = P * PACK
 HALF = F // 2
 RAW_BUFS = 10
-GROUPED_BUFS = 6
-STAGE_BUFS = 7
+GROUPED_BUFS = 4
+STAGE_BUFS = 9
 
 
 def tile_flow_average_residual_update_k1_kernel(
@@ -67,9 +67,9 @@ def tile_flow_average_residual_update_k1_kernel(
 
         load_order = [
             ("x", 0, 0), ("x", 0, 1), ("wj", 0, 0), ("wj", 1, 0), ("wj", 1, 1), ("wj", 0, 1),
-            ("x", 1, 0), ("x", 1, 1), ("wg", 0, 0), ("dt", 0, 0), ("dt", 0, 1), ("wj", 2, 0), ("wj", 2, 1),
-            ("wg", 1, 0), ("wj", 3, 0), ("wg", 0, 2), ("wj", 3, 1), ("wg", 1, 2), ("wg", 0, 1), ("wg", 1, 1),
-            ("wg", 1, 3), ("wg", 0, 3),
+            ("x", 1, 0), ("x", 1, 1), ("dt", 0, 0), ("dt", 0, 1), ("wj", 2, 0), ("wj", 3, 1), ("wg", 0, 0),
+            ("wj", 2, 1), ("wj", 3, 0), ("wg", 1, 0), ("wg", 0, 2), ("wg", 1, 1), ("wg", 1, 2), ("wg", 0, 1),
+            ("wg", 0, 3), ("wg", 1, 3),
         ]
         waiting = [(key, source(key)) for key in load_order]
         raw = {}
@@ -155,19 +155,19 @@ def tile_flow_average_residual_update_k1_kernel(
             load_next(1)
 
         factors = new_bank([P, PACK, P], 7, BF16)
-        unit_damp = kept([P, PACK, 6], F32, "unit_damp")
+        factor_cols = kept([P, PACK, 10], F32, "factor_cols")
         hu_col = kept([P, PACK, 4], F32, "hu_col")
 
         def turn_factors():
             for t in range(PACK):
                 nc.tensor.transpose(factors[:, t, :], factor_rows[:, t:KP:PACK], ident16[:])
-            nc.scalar.copy(out=unit_damp[:], in_=factors[:, :, 4:10])
+            nc.scalar.copy(out=factor_cols[:], in_=factors[:, :, 0:10])
 
         dt_damped = [kept([P, PACK, F], F32, "dt_damped%d" % g) for g in range(2)]
 
         def turn_dt(g):
             for u in range(2):
-                bank = new_bank([P, F], 2 + u)
+                bank = new_bank([P, F], 2 - 2 * g + u)
                 for a in range(4):
                     words = raw["dt", 0, a // 2][:].bitcast(F32)
                     nc.tensor.transpose(
@@ -180,63 +180,61 @@ def tile_flow_average_residual_update_k1_kernel(
                     t = 2 * u + e
                     nc.scalar.activation(
                         out=dt_damped[g][:, t, :], in_=pairs[:, :, e], func=COPY,
-                        scale=unit_damp[:, t, 4 + g : 5 + g],
+                        scale=factor_cols[:, t, 8 + g : 9 + g],
                     )
 
-        codes, planes = {}, {}
+        codes, planes, staged = {}, {}, {}
 
-        def quantize(key, src):
-            label = "_".join([str(part) for part in key])
-            codes[key] = kept([P, KP], U32, "codes_" + label)
-            planes[key] = kept([P, KP], U8, "planes_" + label)
-            nc.vector.quantize_mx(out=codes[key][:].bitcast(FP8X4), scales=planes[key][:], in_=src[:])
+        def quantize(key, src, t0=0, t1=PACK):
+            if key not in codes:
+                label = "_".join([str(part) for part in key])
+                codes[key] = kept([P, KP], U32, "codes_" + label)
+                planes[key] = kept([P, KP], U8, "planes_" + label)
+            cols = slice(P * t0, P * t1)
+            nc.vector.quantize_mx(out=codes[key][:, cols].bitcast(FP8X4), scales=planes[key][:, cols], in_=src)
 
-        staged = {}
+        def quantize_staged(key, t0=0, t1=PACK):
+            quantize(key, staged[key, t0], t0, t1)
 
-        def lay_weight(key, engine_copy):
-            staged[key] = new_stage()
-            engine_copy(
-                out=staged[key][:].rearrange("p (t mm m j) -> p mm t m j", t=PACK, m=2, j=PACK),
-                in_=raw[key][:].rearrange("p j (mm m t) -> p mm t m j", m=2, t=PACK),
+        laid = {}
+
+        def weight_laid(key, slots):
+            laid[key] = laid.get(key, 0) + slots
+            if laid[key] == PACK:
+                load_next(1)
+
+        def lay_on_scalar(key, t0=0, t1=PACK):
+            tile = new_stage()
+            staged[key, t0] = tile[:, 0 : (t1 - t0) * KP]
+            nc.scalar.copy(
+                out=staged[key, t0].rearrange("p (t mm m j) -> p mm t m j", mm=P // 2, m=2, j=PACK),
+                in_=raw[key][:].rearrange("p j (mm m t) -> p mm t m j", m=2, t=PACK)[:, :, t0:t1, :, :],
             )
-            load_next(1)
-
-        def quantize_staged(key):
-            quantize(key, staged[key])
-
-        side = {}
+            weight_laid(key, t1 - t0)
 
         def lay_on_gpsimd(pieces):
-            tile = new_side([P, 5 * 2 * KP], BF16)
+            tile = new_side([P, 2 * PACK * KP], BF16)
             col = 0
             for key, t0, t1 in pieces:
                 width = (t1 - t0) * KP
-                side[key, t0] = tile[:, col : col + width]
+                staged[key, t0] = tile[:, col : col + width]
                 nc.gpsimd.tensor_scalar(
-                    out=side[key, t0].rearrange("p (t m j) -> p t m j", m=P, j=PACK),
+                    out=staged[key, t0].rearrange("p (t m j) -> p t m j", m=P, j=PACK),
                     in0=raw[key][:].rearrange("p j (m t) -> p t m j", t=PACK)[:, t0:t1, :, :],
                     scalar1=1.0, scalar2=0.0, op0=MULT, op1=ADD,
                 )
                 col = col + width
-                if t1 == PACK:
-                    load_next(1)
+                weight_laid(key, t1 - t0)
 
         def quantize_side(pieces):
             for key, t0, t1 in pieces:
-                if t0 == 0:
-                    label = "_".join([str(part) for part in key])
-                    codes[key] = kept([P, KP], U32, "codes_" + label)
-                    planes[key] = kept([P, KP], U8, "planes_" + label)
-                cols = slice(P * t0, P * t1)
-                nc.vector.quantize_mx(
-                    out=codes[key][:, cols].bitcast(FP8X4), scales=planes[key][:, cols], in_=side[key, t0]
-                )
+                quantize_staged(key, t0, t1)
 
         banks = {}
-        low, high = [0, 1, 2, 3], [4, 5, 6, 7]
+        low, high = [2, 3, 0, 1], [4, 5, 6, 7]
         bank_of = {
-            (1, 0): [4, 5, 6, 0], (1, 1): [1, 2, 3, 4], (1, 2): [4, 5, 6, 0], (1, 3): [1, 2, 3, 4],
-            (2, 0): low, (2, 1): high, (3, 0): low, (3, 2): high, (3, 1): high, (3, 3): high,
+            (1, 0): [4, 5, 6, 0], (1, 1): [1, 2, 3, 7], (1, 2): high, (1, 3): low,
+            (2, 0): high, (2, 1): low, (3, 0): high, (3, 2): low, (3, 1): low, (3, 3): low,
         }
 
         def passes(stage, unit_key, ks, depth, slots=range(PACK)):
@@ -273,14 +271,7 @@ def tile_flow_average_residual_update_k1_kernel(
                     out=sums[:, t, :], in0=banks[stage, unit_key, t][:], in1=columns[:, :, t], op=ADD
                 )
 
-        def scale_round(key, sums, factor):
-            staged[key] = new_stage()
-            nc.vector.tensor_tensor(
-                out=staged[key][:].rearrange("p (c e t) -> p c t e", e=2, t=PACK),
-                in0=sums.rearrange("p t (c e) -> p c t e", e=2),
-                in1=factor.unsqueeze(1).unsqueeze(3).to_broadcast([P, F // 2, PACK, 2]),
-                op=MULT,
-            )
+        by_slot = {}
 
         def add_x(kk):
             i, g = divmod(kk, 2)
@@ -288,28 +279,37 @@ def tile_flow_average_residual_update_k1_kernel(
 
         def scale_wbar(kk):
             i, g = divmod(kk, 2)
-            scale_round(("wbar", kk), flow[g][:, i, :, :], factors[:, :, kk])
-
-        resid = {}
+            by_slot["wbar", kk] = new_stage()
+            for t in range(PACK):
+                nc.vector.tensor_scalar(
+                    out=by_slot["wbar", kk][:, F * t : F * (t + 1)],
+                    in0=flow[g][:, i, t, :],
+                    scalar1=factor_cols[:, t, kk : kk + 1],
+                    scalar2=None,
+                    op0=MULT,
+                )
 
         def finish_r(g):
-            resid[g] = new_stage()
+            by_slot["r", g] = new_stage()
             for t in range(PACK):
                 nc.vector.scalar_tensor_tensor(
-                    out=resid[g][:, F * t : F * (t + 1)],
+                    out=by_slot["r", g][:, F * t : F * (t + 1)],
                     in0=banks[2, g, t][:],
-                    scalar=unit_damp[:, t, 4 + g : 5 + g],
+                    scalar=factor_cols[:, t, 8 + g : 9 + g],
                     in1=dt_damped[g][:, t, :],
                     op0=MULT,
                     op1=ADD,
                 )
 
-        def lay_r(g, engine_copy):
-            staged["r", g] = new_stage()
-            engine_copy(
-                out=staged["r", g][:].rearrange("p (c e t) -> p c t e", e=4, t=PACK),
-                in_=resid[g][:].rearrange("p (t c e) -> p c t e", t=PACK, e=4),
-            )
+        def lay_slots(key, engine_copies):
+            tile = new_stage()
+            staged[key, 0] = tile[:]
+            dst = tile[:].rearrange("p (c e t) -> p c t e", e=4, t=PACK)
+            src = by_slot[key][:].rearrange("p (t c e) -> p c t e", t=PACK, e=4)
+            share = F // 4 // len(engine_copies)
+            for n, engine_copy in enumerate(engine_copies):
+                part = slice(share * n, share * (n + 1))
+                engine_copy(out=dst[:, part, :, :], in_=src[:, part, :, :])
 
         def finish_y(kk, slots=range(PACK)):
             i, g = divmod(kk, 2)
@@ -327,7 +327,7 @@ def tile_flow_average_residual_update_k1_kernel(
             i, g = divmod(kk, 2)
             rows = new_grouped([P, 2, KP], F32)
             for a in range(2):
-                bank = new_bank([P, PACK, P], 2 * half + a)
+                bank = new_bank([P, PACK, P], 4 + 2 * half + a)
                 f0 = HALF * half + P * a
                 for t in range(PACK):
                     nc.tensor.transpose(bank[:, t, :], flow[g][:, i, t, f0 : f0 + P], ident[:])
@@ -337,11 +337,8 @@ def tile_flow_average_residual_update_k1_kernel(
                 )
             nc.sync.dma_start(out=frame_rows(out_0[:, i, KP * g : KP * (g + 1)], half), in_=rows[:])
 
-        def on_gpsimd(out, in_):
-            nc.gpsimd.tensor_scalar(out=out, in0=in_, scalar1=1.0, scalar2=0.0, op0=MULT, op1=ADD)
-
         def round_y(g, half, engine_copy):
-            staged["y", g, half] = new_side([P, KP * PACK], BF16) if g == 0 else new_stage()
+            staged["y", g, half] = new_stage()
             engine_copy(
                 out=staged["y", g, half][:].rearrange("p (c e s) -> p c s e", e=2, s=U * PACK),
                 in_=flow[g][:, :, :, HALF * half : HALF * (half + 1)].rearrange(
@@ -349,32 +346,33 @@ def tile_flow_average_residual_update_k1_kernel(
                 ),
             )
 
-        y_planes = [kept([P, F * U], U8, "y_planes%d" % g) for g in range(2)]
+        y_planes = kept([P, F * U], U8, "y_planes")
 
         def quantize_y(g, half):
             y_codes = kept([P, KP], U32, "y_codes%d_%d" % (g, half))
             cols = slice(KP * half, KP * (half + 1))
             nc.vector.quantize_mx(
-                out=y_codes[:].bitcast(FP8X4), scales=y_planes[g][:, cols], in_=staged["y", g, half][:]
+                out=y_codes[:].bitcast(FP8X4), scales=y_planes[4 * g : P, cols], in_=staged["y", g, half][:]
             )
             nc.sync.dma_start(
                 out=out_1[g].rearrange("p m t -> p (m t)").bitcast(I32)[:, cols], in_=y_codes[:].bitcast(I32)
             )
 
-        def store_y_planes(g):
+        def store_y_planes():
             for q in range(4):
                 nc.sync.dma_start(
-                    out=out_2[g, 4 * q : 4 * q + 4, :].bitcast(I32),
-                    in_=y_planes[g][32 * q : 32 * q + 4, :].bitcast(I32),
+                    out=out_2[:, 4 * q : 4 * q + 4, :].bitcast(I32),
+                    in_=y_planes[32 * q : 32 * q + 8, :].bitcast(I32),
                 )
 
         on_scalar = nc.scalar.copy
         on_vector = nc.vector.tensor_copy
 
         side_work = [
-            [(("wj", 1, 0), 0, 4), (("wj", 1, 1), 0, 4), (("wg", 0, 0), 0, 2)],
-            [(("wg", 0, 0), 2, 4), (("wg", 1, 0), 0, 4), (("wg", 0, 2), 0, 4)],
-            [(("wg", 1, 3), 0, 4)],
+            [(("wj", 1, 0), 0, 4), (("wj", 1, 1), 0, 4)],
+            [(("wj", 3, 1), 0, 4), (("wg", 0, 0), 0, 2)],
+            [(("wg", 0, 2), 0, 4), (("wg", 1, 1), 0, 2)],
+            [(("wg", 0, 3), 0, 4), (("wg", 1, 3), 0, 2)],
         ]
         order_d_codes(0, [0, 1])
         turn("x", 0, 0, [0, 1])
@@ -383,103 +381,106 @@ def tile_flow_average_residual_update_k1_kernel(
         turn_factors()
         order_d_scales(1)
         order_d_codes(1, [0])
-        quantize(("x", 0, 0), grouped["x", 0, 0])
-        quantize(("x", 0, 1), grouped["x", 0, 1])
+        quantize(("x", 0, 0), grouped["x", 0, 0][:])
+        quantize(("x", 0, 1), grouped["x", 0, 1][:])
         passes(1, 0, [0], 2)
         passes(1, 0, [1], 2)
         order_d_codes(1, [1])
-        lay_weight(("wj", 0, 0), on_scalar)
+        lay_on_scalar(("wj", 0, 0))
         lay_on_gpsimd(side_work[0])
-        lay_weight(("wj", 0, 1), on_scalar)
-        passes(1, 1, [0, 1], 2, range(3))
+        lay_on_scalar(("wj", 0, 1))
+        passes(1, 1, [0, 1], 2)
         add_x(0)
-        passes(1, 1, [0, 1], 2, [3])
-        turn("x", 1, 0, [5, 6])
+        turn("x", 1, 0, [4, 5])
+        turn("x", 1, 1, [6, 0])
         add_x(1)
-        turn("x", 1, 1, [0, 1])
+        scale_wbar(0)
+        lay_slots(("wbar", 0), [on_scalar])
+        scale_wbar(1)
         turn_dt(0)
         turn_dt(1)
         load_next(2)
-        scale_wbar(0)
-        scale_wbar(1)
-        nc.vector.tensor_tensor(out=hu_col[:], in0=factors[:, :, 0:4], in1=unit_damp[:, :, 0:4], op=MULT)
-        quantize(("x", 1, 0), grouped["x", 1, 0])
-        quantize(("x", 1, 1), grouped["x", 1, 1])
+        nc.vector.tensor_tensor(out=hu_col[:], in0=factor_cols[:, :, 0:4], in1=factor_cols[:, :, 4:8], op=MULT)
+        quantize(("x", 1, 0), grouped["x", 1, 0][:])
+        quantize(("x", 1, 1), grouped["x", 1, 1][:])
         passes(1, 2, [0, 1], 2)
-        passes(1, 3, [0, 1], 2, range(3))
+        passes(1, 3, [0, 1], 2)
+        lay_slots(("wbar", 1), [on_scalar])
         quantize_staged(("wj", 0, 0))
         quantize_staged(("wj", 0, 1))
         quantize_staged(("wbar", 0))
-        quantize_staged(("wbar", 1))
-        lay_weight(("wj", 2, 0), on_scalar)
-        lay_weight(("wj", 2, 1), on_scalar)
-        lay_weight(("wj", 3, 0), on_scalar)
-        lay_weight(("wj", 3, 1), on_scalar)
+        lay_on_scalar(("wj", 2, 0))
+        lay_on_scalar(("wj", 2, 1))
+        lay_on_scalar(("wj", 3, 0))
         quantize_side(side_work[0])
         lay_on_gpsimd(side_work[1])
         add_x(2)
-        passes(1, 3, [0, 1], 2, [3])
         add_x(3)
-        passes(2, 0, [0, 1], 4)
-        passes(2, 1, [0, 1], 4, range(3))
         scale_wbar(2)
+        quantize_staged(("wbar", 1))
+        passes(2, 0, [0, 1], 4)
+        passes(2, 1, [0, 1], 4)
         scale_wbar(3)
-        passes(2, 1, [0, 1], 4, [3])
+        lay_slots(("wbar", 2), [on_vector])
+        lay_slots(("wbar", 3), [on_vector])
         quantize_staged(("wj", 2, 0))
         quantize_staged(("wbar", 2))
         passes(2, 0, [2], 4)
-        lay_weight(("wg", 1, 2), on_scalar)
-        lay_weight(("wg", 0, 1), on_scalar)
-        quantize_staged(("wj", 3, 0))
-        quantize_staged(("wbar", 3))
-        passes(2, 0, [3], 4)
+        lay_on_scalar(("wg", 0, 0), 2, 4)
         quantize_staged(("wj", 2, 1))
-        quantize_staged(("wj", 3, 1))
-        passes(2, 1, [2, 3], 4)
-        lay_weight(("wg", 1, 1), on_scalar)
+        passes(2, 1, [2], 4)
+        lay_on_scalar(("wg", 1, 0))
+        quantize_staged(("wbar", 3))
+        quantize_staged(("wj", 3, 0))
+        passes(2, 0, [3], 4)
         quantize_side(side_work[1])
+        passes(2, 1, [3], 4)
         lay_on_gpsimd(side_work[2])
+        lay_on_scalar(("wg", 1, 2))
         finish_r(0)
-        lay_r(0, on_scalar)
+        lay_slots(("r", 0), [on_scalar])
         finish_r(1)
-        lay_r(1, on_scalar)
-        quantize_staged(("wg", 1, 2))
-        lay_weight(("wg", 0, 3), on_scalar)
-        quantize_staged(("wg", 0, 1))
+        lay_slots(("r", 1), [on_scalar, on_vector])
+        lay_on_scalar(("wg", 0, 1))
+        lay_on_scalar(("wg", 1, 1), 2, 4)
+        lay_on_scalar(("wg", 1, 3), 2, 4)
+        quantize_staged(("wg", 0, 0), 2, 4)
         quantize_staged(("r", 0))
         passes(3, 0, [0], 2)
-        passes(3, 2, [0], 2)
-        quantize_staged(("wg", 1, 1))
+        quantize_staged(("wg", 1, 0))
         quantize_staged(("r", 1))
         passes(3, 0, [1], 2)
-        passes(3, 2, [1], 2)
-        quantize_side(side_work[2])
+        quantize_staged(("wg", 0, 2))
+        quantize_staged(("wg", 1, 2))
+        passes(3, 2, [0, 1], 2)
         finish_y(0)
+        quantize_staged(("wg", 0, 1))
+        quantize_staged(("wg", 1, 1), 2, 4)
+        quantize_staged(("wg", 1, 1), 0, 2)
+        lay_on_gpsimd(side_work[3])
         store_y(0, 0)
-        finish_y(2)
-        passes(3, 1, [0, 1], 2, [0])
         store_y(0, 1)
-        passes(3, 1, [0, 1], 2, [1, 2])
+        finish_y(2)
+        passes(3, 1, [0, 1], 2, [0, 1, 2])
         store_y(2, 0)
         passes(3, 1, [0, 1], 2, [3])
         store_y(2, 1)
-        round_y(0, 0, on_vector)
-        quantize_staged(("wg", 0, 3))
-        quantize_y(0, 0)
-        round_y(0, 1, on_gpsimd)
         finish_y(1)
-        passes(3, 3, [0, 1], 2, [0, 1, 2])
+        quantize_staged(("wg", 1, 3), 2, 4)
+        quantize_side(side_work[3])
         store_y(1, 0)
-        passes(3, 3, [0, 1], 2, [3])
         store_y(1, 1)
+        passes(3, 3, [0, 1], 2)
+        round_y(0, 0, on_vector)
+        round_y(0, 1, on_scalar)
         finish_y(3, [0, 1])
-        quantize_y(0, 1)
-        store_y_planes(0)
+        quantize_y(0, 0)
         finish_y(3, [2, 3])
-        round_y(1, 0, on_vector)
         store_y(3, 0)
+        round_y(1, 0, on_vector)
+        quantize_y(0, 1)
         round_y(1, 1, on_vector)
         store_y(3, 1)
         quantize_y(1, 0)
         quantize_y(1, 1)
-        store_y_planes(1)
+        store_y_planes()

@@ -24,7 +24,7 @@ KP = P * PACK
 HALF = F // 2
 RAW_BUFS = 10
 GROUPED_BUFS = 4
-STAGE_BUFS = 9
+STAGE_BUFS = 8
 
 
 def tile_flow_average_residual_update_k1_kernel(
@@ -67,9 +67,9 @@ def tile_flow_average_residual_update_k1_kernel(
 
         load_order = [
             ("x", 0, 0), ("x", 0, 1), ("wj", 0, 0), ("wj", 1, 0), ("wj", 1, 1), ("wj", 0, 1),
-            ("x", 1, 0), ("x", 1, 1), ("dt", 0, 0), ("dt", 0, 1), ("wj", 2, 0), ("wj", 3, 1), ("wg", 0, 0),
-            ("wj", 2, 1), ("wj", 3, 0), ("wg", 1, 0), ("wg", 0, 2), ("wg", 1, 1), ("wg", 1, 2), ("wg", 0, 1),
-            ("wg", 0, 3), ("wg", 1, 3),
+            ("x", 1, 0), ("x", 1, 1), ("wg", 0, 0), ("dt", 0, 0), ("dt", 0, 1), ("wj", 2, 0), ("wj", 2, 1),
+            ("wg", 1, 0), ("wj", 3, 0), ("wg", 0, 2), ("wj", 3, 1), ("wg", 1, 2), ("wg", 1, 1), ("wg", 0, 1),
+            ("wg", 1, 3), ("wg", 0, 3),
         ]
         waiting = [(key, source(key)) for key in load_order]
         raw = {}
@@ -213,7 +213,7 @@ def tile_flow_average_residual_update_k1_kernel(
             weight_laid(key, t1 - t0)
 
         def lay_on_gpsimd(pieces):
-            tile = new_side([P, 2 * PACK * KP], BF16)
+            tile = new_side([P, 5 * 2 * KP], BF16)
             col = 0
             for key, t0, t1 in pieces:
                 width = (t1 - t0) * KP
@@ -233,8 +233,8 @@ def tile_flow_average_residual_update_k1_kernel(
         banks = {}
         low, high = [2, 3, 0, 1], [4, 5, 6, 7]
         bank_of = {
-            (1, 0): [4, 5, 6, 0], (1, 1): [1, 2, 3, 7], (1, 2): high, (1, 3): low,
-            (2, 0): high, (2, 1): low, (3, 0): high, (3, 2): low, (3, 1): low, (3, 3): low,
+            (1, 0): [4, 5, 6, 0], (1, 1): [1, 2, 3, 4], (1, 2): [4, 5, 6, 2], (1, 3): [3, 0, 1, 4],
+            (2, 0): low, (2, 1): high, (3, 0): low, (3, 2): high, (3, 1): high, (3, 3): high,
         }
 
         def passes(stage, unit_key, ks, depth, slots=range(PACK)):
@@ -279,15 +279,14 @@ def tile_flow_average_residual_update_k1_kernel(
 
         def scale_wbar(kk):
             i, g = divmod(kk, 2)
-            by_slot["wbar", kk] = new_stage()
-            for t in range(PACK):
-                nc.vector.tensor_scalar(
-                    out=by_slot["wbar", kk][:, F * t : F * (t + 1)],
-                    in0=flow[g][:, i, t, :],
-                    scalar1=factor_cols[:, t, kk : kk + 1],
-                    scalar2=None,
-                    op0=MULT,
-                )
+            tile = new_stage()
+            staged[("wbar", kk), 0] = tile[:]
+            nc.vector.tensor_tensor(
+                out=tile[:].rearrange("p (c e t) -> p c t e", e=2, t=PACK),
+                in0=flow[g][:, i, :, :].rearrange("p t (c e) -> p c t e", e=2),
+                in1=factors[:, :, kk].unsqueeze(1).unsqueeze(3).to_broadcast([P, F // 2, PACK, 2]),
+                op=MULT,
+            )
 
         def finish_r(g):
             by_slot["r", g] = new_stage()
@@ -304,12 +303,12 @@ def tile_flow_average_residual_update_k1_kernel(
         def lay_slots(key, engine_copies):
             tile = new_stage()
             staged[key, 0] = tile[:]
-            dst = tile[:].rearrange("p (c e t) -> p c t e", e=4, t=PACK)
-            src = by_slot[key][:].rearrange("p (t c e) -> p c t e", t=PACK, e=4)
-            share = F // 4 // len(engine_copies)
+            dst = tile[:].rearrange("p (f t) -> p f t", t=PACK)
+            src = by_slot[key][:].rearrange("p (t f) -> p f t", t=PACK)
+            share = F // len(engine_copies)
             for n, engine_copy in enumerate(engine_copies):
                 part = slice(share * n, share * (n + 1))
-                engine_copy(out=dst[:, part, :, :], in_=src[:, part, :, :])
+                engine_copy(out=dst[:, part, :], in_=src[:, part, :])
 
         def finish_y(kk, slots=range(PACK)):
             i, g = divmod(kk, 2)
@@ -327,7 +326,7 @@ def tile_flow_average_residual_update_k1_kernel(
             i, g = divmod(kk, 2)
             rows = new_grouped([P, 2, KP], F32)
             for a in range(2):
-                bank = new_bank([P, PACK, P], 4 + 2 * half + a)
+                bank = new_bank([P, PACK, P], 2 - 2 * half + a)
                 f0 = HALF * half + P * a
                 for t in range(PACK):
                     nc.tensor.transpose(bank[:, t, :], flow[g][:, i, t, f0 : f0 + P], ident[:])
@@ -340,9 +339,9 @@ def tile_flow_average_residual_update_k1_kernel(
         def round_y(g, half, engine_copy):
             staged["y", g, half] = new_stage()
             engine_copy(
-                out=staged["y", g, half][:].rearrange("p (c e s) -> p c s e", e=2, s=U * PACK),
+                out=staged["y", g, half][:].rearrange("p (c e i t) -> p c i e t", e=2, i=U, t=PACK),
                 in_=flow[g][:, :, :, HALF * half : HALF * (half + 1)].rearrange(
-                    "p i t (c e) -> p c (i t) e", e=2
+                    "p i t (c e) -> p c i e t", e=2
                 ),
             )
 
@@ -369,10 +368,10 @@ def tile_flow_average_residual_update_k1_kernel(
         on_vector = nc.vector.tensor_copy
 
         side_work = [
-            [(("wj", 1, 0), 0, 4), (("wj", 1, 1), 0, 4)],
-            [(("wj", 3, 1), 0, 4), (("wg", 0, 0), 0, 2)],
-            [(("wg", 0, 2), 0, 4), (("wg", 1, 1), 0, 2)],
-            [(("wg", 0, 3), 0, 4), (("wg", 1, 3), 0, 2)],
+            [(("wj", 1, 0), 0, 4), (("wj", 1, 1), 0, 4), (("wg", 0, 0), 0, 2)],
+            [(("wg", 0, 0), 2, 4), (("wg", 1, 0), 0, 4), (("wg", 0, 2), 0, 4)],
+            [(("wg", 1, 1), 0, 4)],
+            [(("wg", 0, 3), 0, 4)],
         ]
         order_d_codes(0, [0, 1])
         turn("x", 0, 0, [0, 1])
@@ -389,75 +388,69 @@ def tile_flow_average_residual_update_k1_kernel(
         lay_on_scalar(("wj", 0, 0))
         lay_on_gpsimd(side_work[0])
         lay_on_scalar(("wj", 0, 1))
-        passes(1, 1, [0, 1], 2)
+        passes(1, 1, [0, 1], 2, [0, 1, 2])
         add_x(0)
-        turn("x", 1, 0, [4, 5])
-        turn("x", 1, 1, [6, 0])
+        passes(1, 1, [0, 1], 2, [3])
+        turn("x", 1, 0, [5, 6])
         add_x(1)
-        scale_wbar(0)
-        lay_slots(("wbar", 0), [on_scalar])
-        scale_wbar(1)
+        turn("x", 1, 1, [0, 1])
         turn_dt(0)
         turn_dt(1)
         load_next(2)
-        nc.vector.tensor_tensor(out=hu_col[:], in0=factor_cols[:, :, 0:4], in1=factor_cols[:, :, 4:8], op=MULT)
+        scale_wbar(0)
+        scale_wbar(1)
+        nc.vector.tensor_tensor(out=hu_col[:], in0=factors[:, :, 0:4], in1=factor_cols[:, :, 4:8], op=MULT)
         quantize(("x", 1, 0), grouped["x", 1, 0][:])
         quantize(("x", 1, 1), grouped["x", 1, 1][:])
         passes(1, 2, [0, 1], 2)
-        passes(1, 3, [0, 1], 2)
-        lay_slots(("wbar", 1), [on_scalar])
+        passes(1, 3, [0, 1], 2, [0, 1, 2])
         quantize_staged(("wj", 0, 0))
         quantize_staged(("wj", 0, 1))
         quantize_staged(("wbar", 0))
+        quantize_staged(("wbar", 1))
         lay_on_scalar(("wj", 2, 0))
         lay_on_scalar(("wj", 2, 1))
         lay_on_scalar(("wj", 3, 0))
+        lay_on_scalar(("wj", 3, 1))
         quantize_side(side_work[0])
         lay_on_gpsimd(side_work[1])
         add_x(2)
+        passes(1, 3, [0, 1], 2, [3])
         add_x(3)
-        scale_wbar(2)
-        quantize_staged(("wbar", 1))
         passes(2, 0, [0, 1], 4)
-        passes(2, 1, [0, 1], 4)
+        passes(2, 1, [0, 1], 4, [0, 1, 2])
+        scale_wbar(2)
         scale_wbar(3)
-        lay_slots(("wbar", 2), [on_vector])
-        lay_slots(("wbar", 3), [on_vector])
+        passes(2, 1, [0, 1], 4, [3])
         quantize_staged(("wj", 2, 0))
         quantize_staged(("wbar", 2))
         passes(2, 0, [2], 4)
-        lay_on_scalar(("wg", 0, 0), 2, 4)
-        quantize_staged(("wj", 2, 1))
-        passes(2, 1, [2], 4)
-        lay_on_scalar(("wg", 1, 0))
-        quantize_staged(("wbar", 3))
-        quantize_staged(("wj", 3, 0))
-        passes(2, 0, [3], 4)
-        quantize_side(side_work[1])
-        passes(2, 1, [3], 4)
-        lay_on_gpsimd(side_work[2])
         lay_on_scalar(("wg", 1, 2))
+        lay_on_scalar(("wg", 0, 1))
+        quantize_staged(("wj", 3, 0))
+        quantize_staged(("wbar", 3))
+        passes(2, 0, [3], 4)
+        quantize_staged(("wj", 2, 1))
+        quantize_staged(("wj", 3, 1))
+        passes(2, 1, [2, 3], 4)
+        quantize_side(side_work[1])
+        lay_on_gpsimd(side_work[2])
         finish_r(0)
         lay_slots(("r", 0), [on_scalar])
         finish_r(1)
         lay_slots(("r", 1), [on_scalar, on_vector])
-        lay_on_scalar(("wg", 0, 1))
-        lay_on_scalar(("wg", 1, 1), 2, 4)
-        lay_on_scalar(("wg", 1, 3), 2, 4)
-        quantize_staged(("wg", 0, 0), 2, 4)
+        lay_on_scalar(("wg", 1, 3))
         quantize_staged(("r", 0))
         passes(3, 0, [0], 2)
-        quantize_staged(("wg", 1, 0))
+        passes(3, 2, [0], 2)
+        quantize_staged(("wg", 1, 2))
+        quantize_staged(("wg", 0, 1))
         quantize_staged(("r", 1))
         passes(3, 0, [1], 2)
-        quantize_staged(("wg", 0, 2))
-        quantize_staged(("wg", 1, 2))
-        passes(3, 2, [0, 1], 2)
-        finish_y(0)
-        quantize_staged(("wg", 0, 1))
-        quantize_staged(("wg", 1, 1), 2, 4)
-        quantize_staged(("wg", 1, 1), 0, 2)
+        passes(3, 2, [1], 2)
+        quantize_side(side_work[2])
         lay_on_gpsimd(side_work[3])
+        finish_y(0)
         store_y(0, 0)
         store_y(0, 1)
         finish_y(2)
@@ -466,7 +459,7 @@ def tile_flow_average_residual_update_k1_kernel(
         passes(3, 1, [0, 1], 2, [3])
         store_y(2, 1)
         finish_y(1)
-        quantize_staged(("wg", 1, 3), 2, 4)
+        quantize_staged(("wg", 1, 3))
         quantize_side(side_work[3])
         store_y(1, 0)
         store_y(1, 1)

@@ -20,11 +20,17 @@ COPY = mybir.ActivationFunctionType.Copy
 
 P = 128
 PACK = 4
-KP = P * PACK
+GROUP = P * PACK
 HALF = F // 2
+ALL_SLOTS = range(PACK)
+
 RAW_BUFS = 10
-GROUPED_BUFS = 4
-STAGE_BUFS = 8
+X_BUFS = 4
+STAGE_BUFS = 9
+SIDE_SLOTS = 10
+
+FACTOR_BANK = 7
+UNIT_ROW, DAMP_ROW, FACTOR_ROWS = 4, 8, 10
 
 
 def tile_flow_average_residual_update_k1_kernel(
@@ -44,38 +50,40 @@ def tile_flow_average_residual_update_k1_kernel(
             return psum.tile(shape, dtype, name="bank%d" % number)
 
         def new_stage():
-            return ring.tile([P, KP * PACK], BF16, name="stage", bufs=STAGE_BUFS, align_bytes=64)
+            tile = ring.tile([P, GROUP * PACK], BF16, name="stage", bufs=STAGE_BUFS, align_bytes=64)
+            return tile[:]
 
-        def new_grouped(shape, dtype):
-            return ring.tile(shape, dtype, name="grouped", bufs=GROUPED_BUFS, align_bytes=64)
+        def new_x_or_rows(shape, dtype):
+            return ring.tile(shape, dtype, name="x_or_rows", bufs=X_BUFS, align_bytes=64)
+
+        def new_side(shape, dtype):
+            return ring.tile(shape, dtype, name="side", bufs=1, align_bytes=64)
 
         def frame_rows(src, half):
             return src[HALF * half : HALF * (half + 1), :].rearrange("(a p) n -> p a n", p=P)
 
         def weight_rows(w, k, col):
-            return w[KP * k : KP * (k + 1), col : col + KP].rearrange("(p j) c -> p j c", j=PACK)
+            return w[GROUP * k : GROUP * (k + 1), col : col + GROUP].rearrange("(p j) c -> p j c", j=PACK)
 
         def source(key):
-            name, a, b = key
+            name, first, second = key
             if name == "x":
-                return frame_rows(x[:, a, :], b)
+                return frame_rows(x[:, first, :], second)
             if name == "dt":
-                return frame_rows(dt, b)
-            if name == "wj":
-                return weight_rows(wj, a, KP * b)
-            return weight_rows(wg, a, PIX * (b // 2) + KP * (b % 2))
+                return frame_rows(dt, second)
+            return weight_rows(wj if name == "wj" else wg, first, GROUP * second)
 
         load_order = [
             ("x", 0, 0), ("x", 0, 1), ("wj", 0, 0), ("wj", 1, 0), ("wj", 1, 1), ("wj", 0, 1),
             ("x", 1, 0), ("x", 1, 1), ("wg", 0, 0), ("dt", 0, 0), ("dt", 0, 1), ("wj", 2, 0), ("wj", 2, 1),
-            ("wg", 1, 0), ("wj", 3, 0), ("wg", 0, 2), ("wj", 3, 1), ("wg", 1, 2), ("wg", 1, 1), ("wg", 0, 1),
-            ("wg", 1, 3), ("wg", 0, 3),
+            ("wg", 1, 0), ("wj", 3, 0), ("wg", 0, 2), ("wj", 3, 1), ("wg", 1, 2), ("wg", 0, 1), ("wg", 1, 3),
+            ("wg", 1, 1), ("wg", 0, 3),
         ]
-        waiting = [(key, source(key)) for key in load_order]
         raw = {}
 
         def load_next(count):
-            for key, src in waiting[len(raw) : len(raw) + count]:
+            for key in load_order[len(raw) : len(raw) + count]:
+                src = source(key)
                 raw[key] = ring.tile(list(src.shape), BF16, name="raw", bufs=RAW_BUFS, align_bytes=64)
                 nc.sync.dma_start(out=raw[key][:], in_=src)
 
@@ -84,91 +92,93 @@ def tile_flow_average_residual_update_k1_kernel(
         ident16 = kept([P, P], BF16, "ident16")
         make_identity(nc, ident16[:])
 
-        def new_side(shape, dtype):
-            return ring.tile(shape, dtype, name="side", bufs=1, align_bytes=64)
-
-        d_raw = [kept([P, 2, 2 * KP], U8, "d_raw0"), new_side([P, 2, 2 * KP], U8)]
+        d_raw = [kept([P, 2, 2 * GROUP], U8, "d_raw0"), new_side([P, 2, 2 * GROUP], U8)]
         d_raw_scales = kept([P, 2, PIX], U8, "d_raw_scales")
         nc.vector.memset(d_raw_scales[:].bitcast(I32), 0)
-        factor_rows = kept([P, KP], BF16, "factor_rows")
+        factor_rows = kept([P, GROUP], BF16, "factor_rows")
         nc.vector.memset(factor_rows[:], 0.0)
 
         def load_d(g):
-            src = d_words[:, :, 2 * KP * g : 2 * KP * (g + 1)].rearrange("k p n -> p k n")
+            src = d_words[:, :, 2 * GROUP * g : 2 * GROUP * (g + 1)].rearrange("k p n -> p k n")
             nc.sync.dma_start(out=d_raw[g][:].bitcast(I32), in_=src.bitcast(I32))
 
         load_d(0)
-        for q in range(4):
+        for quad in range(4):
             nc.sync.dma_start(
-                out=d_raw_scales[32 * q : 32 * q + 4, :, :].bitcast(I32),
-                in_=d_scales[:, 4 * q : 4 * q + 4, :].rearrange("k r n -> r k n").bitcast(I32),
+                out=d_raw_scales[32 * quad : 32 * quad + 4, :, :].bitcast(I32),
+                in_=d_scales[:, 4 * quad : 4 * quad + 4, :].rearrange("k r n -> r k n").bitcast(I32),
             )
         load_next(2)
         load_d(1)
-        nc.sync.dma_start(out=factor_rows[0:4, :], in_=h.rearrange("i (g n) -> (i g) n", g=2))
+        nc.sync.dma_start(out=factor_rows[0:UNIT_ROW, :], in_=h.rearrange("i (g n) -> (i g) n", g=2))
         load_next(1)
-        nc.sync.dma_start(out=factor_rows[4:8, :], in_=unit.rearrange("i (g n) -> (i g) n", g=2))
-        nc.sync.dma_start(out=factor_rows[8:10, :], in_=damp.rearrange("(g n) -> g n", g=2))
-        load_next(RAW_BUFS - 3)
+        nc.sync.dma_start(out=factor_rows[UNIT_ROW:DAMP_ROW, :], in_=unit.rearrange("i (g n) -> (i g) n", g=2))
+        nc.sync.dma_start(out=factor_rows[DAMP_ROW:FACTOR_ROWS, :], in_=damp.rearrange("(g n) -> g n", g=2))
+        load_next(RAW_BUFS - len(raw))
 
-        d_codes, d_planes = {}, {}
+        d_codes = [kept([P, 2, PACK, 2 * P], U8, "d_codes%d" % g) for g in range(2)]
+        d_planes = [kept([P, 2, PACK, P], U8, "d_planes%d" % g) for g in range(2)]
 
         def order_d_codes(g, ks):
-            if ks[0] == 0:
-                d_codes[g] = kept([P, 2, PACK, 2 * P], U8, "d_codes%d" % g)
             for k in ks:
                 nc.vector.tensor_copy(
                     out=d_codes[g][:, k, :, :].rearrange("p t (mm m b) -> p mm t m b", m=8, b=2),
-                    in_=d_raw[g][:, k, :].rearrange(
-                        "p (mm m t b) -> p mm t m b", m=8, t=PACK, b=2
-                    ),
+                    in_=d_raw[g][:, k, :].rearrange("p (mm m t b) -> p mm t m b", m=8, t=PACK, b=2),
                 )
 
         def order_d_scales(g):
-            d_planes[g] = kept([P, 2, PACK, P], U8, "d_planes%d" % g)
             nc.vector.tensor_copy(
                 out=d_planes[g][:].rearrange("p k t (mm m) -> p k mm t m", m=16),
-                in_=d_raw_scales[:, :, KP * g : KP * (g + 1)].rearrange(
+                in_=d_raw_scales[:, :, GROUP * g : GROUP * (g + 1)].rearrange(
                     "p k (mm m t) -> p k mm t m", m=16, t=PACK
                 ),
             )
 
-        grouped = {}
+        x_grouped = {}
 
-        def turn(name, i, half, numbers):
-            words = raw[name, i, half][:].bitcast(F32)
-            for k in range(2):
+        def turn_x(i, half, numbers):
+            words = raw["x", i, half][:].bitcast(F32)
+            for g in range(2):
                 if half == 0:
-                    grouped[name, i, k] = new_grouped([P, F * PACK], BF16)
-                bank = new_bank([P, 2, HALF], numbers[k])
+                    x_grouped[i, g] = new_x_or_rows([P, F * PACK], BF16)
+                bank = new_bank([P, 2, HALF], numbers[g])
                 for a in range(2):
                     for u in range(2):
                         nc.tensor.transpose(
                             bank[:, u, P * a : P * (a + 1)],
-                            words[:, a, 2 * P * k + u : 2 * P * (k + 1) : 2],
+                            words[:, a, 2 * P * g + u : 2 * P * (g + 1) : 2],
                             ident[:],
                         )
-                dst = grouped[name, i, k][:].bitcast(F32)[:, 2 * HALF * half : 2 * HALF * (half + 1)]
+                dst = x_grouped[i, g][:].bitcast(F32)[:, 2 * HALF * half : 2 * HALF * (half + 1)]
                 nc.scalar.copy(
-                    out=dst.rearrange("p (r u) -> p r u", u=2), in_=bank[:].rearrange("p u r -> p r u")
+                    out=dst.rearrange("p (f u) -> p f u", u=2), in_=bank[:].rearrange("p u f -> p f u")
                 )
             load_next(1)
 
-        factors = new_bank([P, PACK, P], 7, BF16)
-        factor_cols = kept([P, PACK, 10], F32, "factor_cols")
-        hu_col = kept([P, PACK, 4], F32, "hu_col")
+        factors = new_bank([P, PACK, P], FACTOR_BANK, BF16)
+        unit_damp = kept([P, PACK, FACTOR_ROWS - UNIT_ROW], F32, "unit_damp")
+        h_unit = kept([P, PACK, UNIT_ROW], F32, "h_unit")
 
         def turn_factors():
-            for t in range(PACK):
-                nc.tensor.transpose(factors[:, t, :], factor_rows[:, t:KP:PACK], ident16[:])
-            nc.scalar.copy(out=factor_cols[:], in_=factors[:, :, 0:10])
+            for t in ALL_SLOTS:
+                nc.tensor.transpose(factors[:, t, :], factor_rows[:, t:GROUP:PACK], ident16[:])
+            nc.scalar.copy(out=unit_damp[:], in_=factors[:, :, UNIT_ROW:FACTOR_ROWS])
+
+        def damp_of(g, t):
+            col = DAMP_ROW - UNIT_ROW + g
+            return unit_damp[:, t, col : col + 1]
+
+        def multiply_h_unit():
+            nc.vector.tensor_tensor(
+                out=h_unit[:], in0=factors[:, :, 0:UNIT_ROW], in1=unit_damp[:, :, 0:UNIT_ROW], op=MULT
+            )
 
         dt_damped = [kept([P, PACK, F], F32, "dt_damped%d" % g) for g in range(2)]
 
-        def turn_dt(g):
+        def turn_dt(g, numbers):
             for u in range(2):
-                bank = new_bank([P, F], 2 - 2 * g + u)
-                for a in range(4):
+                bank = new_bank([P, F], numbers[u])
+                for a in range(F // P):
                     words = raw["dt", 0, a // 2][:].bitcast(F32)
                     nc.tensor.transpose(
                         bank[:, P * a : P * (a + 1)],
@@ -179,301 +189,294 @@ def tile_flow_average_residual_update_k1_kernel(
                 for e in range(2):
                     t = 2 * u + e
                     nc.scalar.activation(
-                        out=dt_damped[g][:, t, :], in_=pairs[:, :, e], func=COPY,
-                        scale=factor_cols[:, t, 8 + g : 9 + g],
+                        out=dt_damped[g][:, t, :], in_=pairs[:, :, e], func=COPY, scale=damp_of(g, t)
                     )
 
-        codes, planes, staged = {}, {}, {}
+        codes, planes, grouped = {}, {}, {}
 
-        def quantize(key, src, t0=0, t1=PACK):
+        def quantize(key, part=(0, PACK)):
             if key not in codes:
-                label = "_".join([str(part) for part in key])
-                codes[key] = kept([P, KP], U32, "codes_" + label)
-                planes[key] = kept([P, KP], U8, "planes_" + label)
-            cols = slice(P * t0, P * t1)
-            nc.vector.quantize_mx(out=codes[key][:, cols].bitcast(FP8X4), scales=planes[key][:, cols], in_=src)
-
-        def quantize_staged(key, t0=0, t1=PACK):
-            quantize(key, staged[key, t0], t0, t1)
-
-        laid = {}
-
-        def weight_laid(key, slots):
-            laid[key] = laid.get(key, 0) + slots
-            if laid[key] == PACK:
-                load_next(1)
-
-        def lay_on_scalar(key, t0=0, t1=PACK):
-            tile = new_stage()
-            staged[key, t0] = tile[:, 0 : (t1 - t0) * KP]
-            nc.scalar.copy(
-                out=staged[key, t0].rearrange("p (t mm m j) -> p mm t m j", mm=P // 2, m=2, j=PACK),
-                in_=raw[key][:].rearrange("p j (mm m t) -> p mm t m j", m=2, t=PACK)[:, :, t0:t1, :, :],
+                label = "_".join([str(item) for item in key])
+                codes[key] = kept([P, GROUP], U32, "codes_" + label)
+                planes[key] = kept([P, GROUP], U8, "planes_" + label)
+            cols = slice(P * part[0], P * part[1])
+            nc.vector.quantize_mx(
+                out=codes[key][:, cols].bitcast(FP8X4), scales=planes[key][:, cols], in_=grouped[key, part[0]]
             )
-            weight_laid(key, t1 - t0)
 
-        def lay_on_gpsimd(pieces):
-            tile = new_side([P, 5 * 2 * KP], BF16)
+        def quantize_x(i):
+            for g in range(2):
+                grouped[("x", i, g), 0] = x_grouped[i, g][:]
+                quantize(("x", i, g))
+
+        def lay_on_scalar(key):
+            grouped[key, 0] = new_stage()
+            nc.scalar.copy(
+                out=grouped[key, 0].rearrange("p (t mm m j) -> p mm t m j", t=PACK, m=2, j=PACK),
+                in_=raw[key][:].rearrange("p j (mm m t) -> p mm t m j", m=2, t=PACK),
+            )
+            load_next(1)
+
+        def gpsimd_copy(out, in_):
+            nc.gpsimd.tensor_scalar(out=out, in0=in_, scalar1=1.0, scalar2=0.0, op0=MULT, op1=ADD)
+
+        def lay_on_gpsimd(work):
+            tile = new_side([P, SIDE_SLOTS * GROUP], BF16)
             col = 0
-            for key, t0, t1 in pieces:
-                width = (t1 - t0) * KP
-                staged[key, t0] = tile[:, col : col + width]
-                nc.gpsimd.tensor_scalar(
-                    out=staged[key, t0].rearrange("p (t m j) -> p t m j", m=P, j=PACK),
-                    in0=raw[key][:].rearrange("p j (m t) -> p t m j", t=PACK)[:, t0:t1, :, :],
-                    scalar1=1.0, scalar2=0.0, op0=MULT, op1=ADD,
+            for key, (t0, t1) in work:
+                grouped[key, t0] = tile[:, col : col + (t1 - t0) * GROUP]
+                gpsimd_copy(
+                    grouped[key, t0].rearrange("p (t m j) -> p t m j", m=P, j=PACK),
+                    raw[key][:].rearrange("p j (m t) -> p t m j", t=PACK)[:, t0:t1, :, :],
                 )
-                col = col + width
-                weight_laid(key, t1 - t0)
+                col = col + (t1 - t0) * GROUP
+                if t1 == PACK:
+                    load_next(1)
 
-        def quantize_side(pieces):
-            for key, t0, t1 in pieces:
-                quantize_staged(key, t0, t1)
+        def quantize_side(work):
+            for key, part in work:
+                quantize(key, part)
 
-        banks = {}
         low, high = [2, 3, 0, 1], [4, 5, 6, 7]
         bank_of = {
             (1, 0): [4, 5, 6, 0], (1, 1): [1, 2, 3, 4], (1, 2): [4, 5, 6, 2], (1, 3): [3, 0, 1, 4],
             (2, 0): low, (2, 1): high, (3, 0): low, (3, 2): high, (3, 1): high, (3, 3): high,
         }
+        depth = {1: PIX // GROUP, 2: U * PIX // GROUP, 3: C // GROUP}
+        banks = {}
 
-        def passes(stage, unit_key, ks, depth, slots=range(PACK)):
+        def passes(stage, out_group, ks, slots=ALL_SLOTS):
             for t in slots:
                 if ks[0] == 0:
-                    banks[stage, unit_key, t] = new_bank([P, F], bank_of[stage, unit_key][t])
+                    banks[stage, out_group, t] = new_bank([P, F], bank_of[stage, out_group][t])
                 for k in ks:
                     if stage == 1:
-                        i, g = divmod(unit_key, 2)
+                        i, g = divmod(out_group, 2)
                         lhs = d_codes[g][:, k, t, :].bitcast(FP4X4)
                         lhs_scale = d_planes[g][:, k, t, :]
                         moving = ("x", i, k)
                     else:
-                        wkey = ("wj" if stage == 2 else "wg", k, unit_key)
-                        lhs = codes[wkey][:, P * t : P * (t + 1)].bitcast(FP8X4)
-                        lhs_scale = planes[wkey][:, P * t : P * (t + 1)]
+                        weight = ("wj" if stage == 2 else "wg", k, out_group)
+                        lhs = codes[weight][:, P * t : P * (t + 1)].bitcast(FP8X4)
+                        lhs_scale = planes[weight][:, P * t : P * (t + 1)]
                         moving = ("wbar" if stage == 2 else "r", k)
                     nc.tensor.matmul_mx(
-                        out=banks[stage, unit_key, t][:],
+                        out=banks[stage, out_group, t][:],
                         lhsT=lhs,
                         lhsT_scale=lhs_scale,
                         rhs=codes[moving][:].bitcast(FP8X4),
                         rhs_scale=planes[moving][:],
                         start=(k == 0),
-                        stop=(k == depth - 1),
+                        stop=(k == depth[stage] - 1),
                     )
 
         flow = [kept([P, U, PACK, F], F32, "flow%d" % g) for g in range(2)]
 
-        def add_input(stage, unit_key, sums, addend):
-            columns = addend[:].rearrange("p (f t) -> p f t", t=PACK)
-            for t in range(PACK):
+        def add_x(n):
+            i, g = divmod(n, 2)
+            columns = x_grouped[i, g][:].rearrange("p (f t) -> p f t", t=PACK)
+            for t in ALL_SLOTS:
                 nc.vector.tensor_tensor(
-                    out=sums[:, t, :], in0=banks[stage, unit_key, t][:], in1=columns[:, :, t], op=ADD
+                    out=flow[g][:, i, t, :], in0=banks[1, n, t][:], in1=columns[:, :, t], op=ADD
                 )
 
-        by_slot = {}
-
-        def add_x(kk):
-            i, g = divmod(kk, 2)
-            add_input(1, kk, flow[g][:, i, :, :], grouped["x", i, g])
-
-        def scale_wbar(kk):
-            i, g = divmod(kk, 2)
-            tile = new_stage()
-            staged[("wbar", kk), 0] = tile[:]
+        def scale_wbar(n):
+            i, g = divmod(n, 2)
+            grouped[("wbar", n), 0] = new_stage()
             nc.vector.tensor_tensor(
-                out=tile[:].rearrange("p (c e t) -> p c t e", e=2, t=PACK),
+                out=grouped[("wbar", n), 0].rearrange("p (c e t) -> p c t e", e=2, t=PACK),
                 in0=flow[g][:, i, :, :].rearrange("p t (c e) -> p c t e", e=2),
-                in1=factors[:, :, kk].unsqueeze(1).unsqueeze(3).to_broadcast([P, F // 2, PACK, 2]),
+                in1=factors[:, :, n].unsqueeze(1).unsqueeze(3).to_broadcast([P, F // 2, PACK, 2]),
                 op=MULT,
             )
 
+        r_by_slot = {}
+
         def finish_r(g):
-            by_slot["r", g] = new_stage()
-            for t in range(PACK):
+            r_by_slot[g] = new_stage()
+            for t in ALL_SLOTS:
                 nc.vector.scalar_tensor_tensor(
-                    out=by_slot["r", g][:, F * t : F * (t + 1)],
+                    out=r_by_slot[g][:, F * t : F * (t + 1)],
                     in0=banks[2, g, t][:],
-                    scalar=factor_cols[:, t, 8 + g : 9 + g],
+                    scalar=damp_of(g, t),
                     in1=dt_damped[g][:, t, :],
                     op0=MULT,
                     op1=ADD,
                 )
 
-        def lay_slots(key, engine_copies):
-            tile = new_stage()
-            staged[key, 0] = tile[:]
-            dst = tile[:].rearrange("p (f t) -> p f t", t=PACK)
-            src = by_slot[key][:].rearrange("p (t f) -> p f t", t=PACK)
-            share = F // len(engine_copies)
-            for n, engine_copy in enumerate(engine_copies):
-                part = slice(share * n, share * (n + 1))
-                engine_copy(out=dst[:, part, :], in_=src[:, part, :])
+        def group_r(g, copies):
+            grouped[("r", g), 0] = new_stage()
+            dst = grouped[("r", g), 0].rearrange("p (f t) -> p f t", t=PACK)
+            src = r_by_slot[g].rearrange("p (t f) -> p f t", t=PACK)
+            share = F // len(copies)
+            for turn, copy in enumerate(copies):
+                frames = slice(share * turn, share * (turn + 1))
+                copy(out=dst[:, frames, :], in_=src[:, frames, :])
 
-        def finish_y(kk, slots=range(PACK)):
-            i, g = divmod(kk, 2)
-            for t in slots:
+        def finish_y(n):
+            i, g = divmod(n, 2)
+            for t in ALL_SLOTS:
                 nc.vector.scalar_tensor_tensor(
                     out=flow[g][:, i, t, :],
                     in0=flow[g][:, i, t, :],
-                    scalar=hu_col[:, t, kk : kk + 1],
-                    in1=banks[3, kk, t][:],
+                    scalar=h_unit[:, t, n : n + 1],
+                    in1=banks[3, n, t][:],
                     op0=MULT,
                     op1=SUB,
                 )
 
-        def store_y(kk, half):
-            i, g = divmod(kk, 2)
-            rows = new_grouped([P, 2, KP], F32)
+        def store_y(n, half):
+            i, g = divmod(n, 2)
+            rows = new_x_or_rows([P, 2, GROUP], F32)
             for a in range(2):
-                bank = new_bank([P, PACK, P], 2 - 2 * half + a)
+                bank = new_bank([P, PACK, P], low[2 * half + a])
                 f0 = HALF * half + P * a
-                for t in range(PACK):
+                for t in ALL_SLOTS:
                     nc.tensor.transpose(bank[:, t, :], flow[g][:, i, t, f0 : f0 + P], ident[:])
                 nc.scalar.copy(
                     out=rows[:, a, :].rearrange("p (m t) -> p m t", t=PACK),
                     in_=bank[:].rearrange("p t m -> p m t"),
                 )
-            nc.sync.dma_start(out=frame_rows(out_0[:, i, KP * g : KP * (g + 1)], half), in_=rows[:])
+            nc.sync.dma_start(out=frame_rows(out_0[:, i, GROUP * g : GROUP * (g + 1)], half), in_=rows[:])
 
-        def round_y(g, half, engine_copy):
-            staged["y", g, half] = new_stage()
-            engine_copy(
-                out=staged["y", g, half][:].rearrange("p (c e i t) -> p c i e t", e=2, i=U, t=PACK),
-                in_=flow[g][:, :, :, HALF * half : HALF * (half + 1)].rearrange(
-                    "p i t (c e) -> p c i e t", e=2
-                ),
+        y_grouped = {}
+
+        def round_y(g, half, copy, tile):
+            y_grouped[g, half] = tile
+            copy(
+                out=tile.rearrange("p (c e s) -> p c s e", e=2, s=U * PACK),
+                in_=flow[g][:, :, :, HALF * half : HALF * (half + 1)].rearrange("p i t (c e) -> p c (i t) e", e=2),
             )
 
-        y_planes = kept([P, F * U], U8, "y_planes")
+        y_planes = [kept([P, F * U], U8, "y_planes%d" % g) for g in range(2)]
 
         def quantize_y(g, half):
-            y_codes = kept([P, KP], U32, "y_codes%d_%d" % (g, half))
-            cols = slice(KP * half, KP * (half + 1))
+            y_codes = kept([P, HALF * U], U32, "y_codes%d_%d" % (g, half))
+            cols = slice(HALF * U * half, HALF * U * (half + 1))
             nc.vector.quantize_mx(
-                out=y_codes[:].bitcast(FP8X4), scales=y_planes[4 * g : P, cols], in_=staged["y", g, half][:]
+                out=y_codes[:].bitcast(FP8X4), scales=y_planes[g][:, cols], in_=y_grouped[g, half]
             )
             nc.sync.dma_start(
                 out=out_1[g].rearrange("p m t -> p (m t)").bitcast(I32)[:, cols], in_=y_codes[:].bitcast(I32)
             )
 
-        def store_y_planes():
-            for q in range(4):
+        def store_y_planes(g):
+            for quad in range(4):
                 nc.sync.dma_start(
-                    out=out_2[:, 4 * q : 4 * q + 4, :].bitcast(I32),
-                    in_=y_planes[32 * q : 32 * q + 8, :].bitcast(I32),
+                    out=out_2[g, 4 * quad : 4 * quad + 4, :].bitcast(I32),
+                    in_=y_planes[g][32 * quad : 32 * quad + 4, :].bitcast(I32),
                 )
 
         on_scalar = nc.scalar.copy
         on_vector = nc.vector.tensor_copy
 
+        whole, front, back = (0, PACK), (0, 2), (2, PACK)
         side_work = [
-            [(("wj", 1, 0), 0, 4), (("wj", 1, 1), 0, 4), (("wg", 0, 0), 0, 2)],
-            [(("wg", 0, 0), 2, 4), (("wg", 1, 0), 0, 4), (("wg", 0, 2), 0, 4)],
-            [(("wg", 1, 1), 0, 4)],
-            [(("wg", 0, 3), 0, 4)],
+            [(("wj", 1, 0), whole), (("wj", 1, 1), whole), (("wg", 0, 0), front)],
+            [(("wg", 0, 0), back), (("wg", 1, 0), whole), (("wg", 0, 2), whole)],
+            [(("wg", 1, 3), whole)],
         ]
+
         order_d_codes(0, [0, 1])
-        turn("x", 0, 0, [0, 1])
+        turn_x(0, 0, [0, 1])
         order_d_scales(0)
-        turn("x", 0, 1, [2, 3])
+        turn_x(0, 1, [2, 3])
         turn_factors()
         order_d_scales(1)
         order_d_codes(1, [0])
-        quantize(("x", 0, 0), grouped["x", 0, 0][:])
-        quantize(("x", 0, 1), grouped["x", 0, 1][:])
-        passes(1, 0, [0], 2)
-        passes(1, 0, [1], 2)
+        quantize_x(0)
+        passes(1, 0, [0])
+        passes(1, 0, [1])
         order_d_codes(1, [1])
+
         lay_on_scalar(("wj", 0, 0))
         lay_on_gpsimd(side_work[0])
         lay_on_scalar(("wj", 0, 1))
-        passes(1, 1, [0, 1], 2, [0, 1, 2])
+        passes(1, 1, [0, 1], [0, 1, 2])
         add_x(0)
-        passes(1, 1, [0, 1], 2, [3])
-        turn("x", 1, 0, [5, 6])
+        passes(1, 1, [0, 1], [3])
+        turn_x(1, 0, [5, 6])
         add_x(1)
-        turn("x", 1, 1, [0, 1])
-        turn_dt(0)
-        turn_dt(1)
+        turn_x(1, 1, [0, 1])
+        turn_dt(0, low[0:2])
+        turn_dt(1, low[2:4])
         load_next(2)
         scale_wbar(0)
         scale_wbar(1)
-        nc.vector.tensor_tensor(out=hu_col[:], in0=factors[:, :, 0:4], in1=factor_cols[:, :, 4:8], op=MULT)
-        quantize(("x", 1, 0), grouped["x", 1, 0][:])
-        quantize(("x", 1, 1), grouped["x", 1, 1][:])
-        passes(1, 2, [0, 1], 2)
-        passes(1, 3, [0, 1], 2, [0, 1, 2])
-        quantize_staged(("wj", 0, 0))
-        quantize_staged(("wj", 0, 1))
-        quantize_staged(("wbar", 0))
-        quantize_staged(("wbar", 1))
-        lay_on_scalar(("wj", 2, 0))
-        lay_on_scalar(("wj", 2, 1))
-        lay_on_scalar(("wj", 3, 0))
-        lay_on_scalar(("wj", 3, 1))
+        multiply_h_unit()
+
+        quantize_x(1)
+        passes(1, 2, [0, 1])
+        passes(1, 3, [0, 1], [0, 1, 2])
+        for key in [("wj", 0, 0), ("wj", 0, 1), ("wbar", 0), ("wbar", 1)]:
+            quantize(key)
+        for key in [("wj", 2, 0), ("wj", 2, 1), ("wj", 3, 0), ("wj", 3, 1)]:
+            lay_on_scalar(key)
         quantize_side(side_work[0])
+
         lay_on_gpsimd(side_work[1])
         add_x(2)
-        passes(1, 3, [0, 1], 2, [3])
+        passes(1, 3, [0, 1], [3])
         add_x(3)
-        passes(2, 0, [0, 1], 4)
-        passes(2, 1, [0, 1], 4, [0, 1, 2])
+        passes(2, 0, [0, 1])
+        passes(2, 1, [0, 1], [0, 1, 2])
         scale_wbar(2)
         scale_wbar(3)
-        passes(2, 1, [0, 1], 4, [3])
-        quantize_staged(("wj", 2, 0))
-        quantize_staged(("wbar", 2))
-        passes(2, 0, [2], 4)
+        passes(2, 1, [0, 1], [3])
+
+        quantize(("wj", 2, 0))
+        quantize(("wbar", 2))
+        passes(2, 0, [2])
         lay_on_scalar(("wg", 1, 2))
         lay_on_scalar(("wg", 0, 1))
-        quantize_staged(("wj", 3, 0))
-        quantize_staged(("wbar", 3))
-        passes(2, 0, [3], 4)
-        quantize_staged(("wj", 2, 1))
-        quantize_staged(("wj", 3, 1))
-        passes(2, 1, [2, 3], 4)
+        quantize(("wj", 3, 0))
+        quantize(("wbar", 3))
+        passes(2, 0, [3])
+        quantize(("wj", 2, 1))
+        quantize(("wj", 3, 1))
+        passes(2, 1, [2, 3])
         quantize_side(side_work[1])
+
         lay_on_gpsimd(side_work[2])
         finish_r(0)
-        lay_slots(("r", 0), [on_scalar])
+        group_r(0, [on_scalar])
         finish_r(1)
-        lay_slots(("r", 1), [on_scalar, on_vector])
-        lay_on_scalar(("wg", 1, 3))
-        quantize_staged(("r", 0))
-        passes(3, 0, [0], 2)
-        passes(3, 2, [0], 2)
-        quantize_staged(("wg", 1, 2))
-        quantize_staged(("wg", 0, 1))
-        quantize_staged(("r", 1))
-        passes(3, 0, [1], 2)
-        passes(3, 2, [1], 2)
-        quantize_side(side_work[2])
-        lay_on_gpsimd(side_work[3])
+        group_r(1, [on_scalar, on_vector])
+        lay_on_scalar(("wg", 1, 1))
+        lay_on_scalar(("wg", 0, 3))
+        quantize(("r", 0))
+        passes(3, 0, [0])
+        quantize(("wg", 1, 2))
+        quantize(("r", 1))
+        passes(3, 0, [1])
+        passes(3, 2, [0, 1])
+        quantize(("wg", 0, 1))
+
         finish_y(0)
         store_y(0, 0)
         store_y(0, 1)
+        quantize(("wg", 1, 1))
         finish_y(2)
-        passes(3, 1, [0, 1], 2, [0, 1, 2])
-        store_y(2, 0)
-        passes(3, 1, [0, 1], 2, [3])
-        store_y(2, 1)
-        finish_y(1)
-        quantize_staged(("wg", 1, 3))
-        quantize_side(side_work[3])
-        store_y(1, 0)
-        store_y(1, 1)
-        passes(3, 3, [0, 1], 2)
-        round_y(0, 0, on_vector)
-        round_y(0, 1, on_scalar)
-        finish_y(3, [0, 1])
+        quantize(("wg", 0, 3))
+        round_y(0, 0, on_vector, new_stage())
+        quantize_side(side_work[2])
+
+        side_tile = new_side([P, PACK * GROUP], BF16)
+        round_y(0, 1, gpsimd_copy, side_tile[:])
+        for n, done in [(1, 2), (3, 1)]:
+            passes(3, n, [0, 1], [0, 1, 2])
+            store_y(done, 0)
+            passes(3, n, [0, 1], [3])
+            store_y(done, 1)
+            finish_y(n)
+
         quantize_y(0, 0)
-        finish_y(3, [2, 3])
-        store_y(3, 0)
-        round_y(1, 0, on_vector)
+        round_y(1, 0, on_vector, new_stage())
         quantize_y(0, 1)
-        round_y(1, 1, on_vector)
+        store_y_planes(0)
+        store_y(3, 0)
+        round_y(1, 1, on_vector, new_stage())
         store_y(3, 1)
         quantize_y(1, 0)
         quantize_y(1, 1)
-        store_y_planes()
+        store_y_planes(1)

from contextlib import ExitStack

import concourse.mybir as mybir
from concourse.masks import make_identity

F, U, PIX, C = 512, 2, 1024, 1024
FLOPS = 2 * (F * U) * PIX * PIX + 2 * F * (U * PIX) * C + 2 * F * C * (U * PIX)

F32 = mybir.dt.float32
BF16 = mybir.dt.bfloat16
I32 = mybir.dt.int32
U32 = mybir.dt.uint32
U8 = mybir.dt.uint8
FP8X4 = mybir.dt.float8_e4m3fn_x4
FP4X4 = mybir.dt.float4_e2m1fn_x4
ADD = mybir.AluOpType.add
MULT = mybir.AluOpType.mult
SUB = mybir.AluOpType.subtract
COPY = mybir.ActivationFunctionType.Copy

P = 128
PACK = 4
GROUP = P * PACK
HALF = F // 2
ALL_SLOTS = range(PACK)

RAW_BUFS = 10
X_BUFS = 4
STAGE_BUFS = 9
SIDE_SLOTS = 10

FACTOR_BANK = 7
UNIT_ROW, DAMP_ROW, FACTOR_ROWS = 4, 8, 10


def tile_flow_average_residual_update_k1_kernel(
    tc, x, d_words, d_scales, h, wj, dt, damp, wg, unit, out_0, out_1, out_2
):
    nc = tc.nc
    with ExitStack() as ctx:
        keep = ctx.enter_context(tc.tile_pool(name="keep", bufs=1))
        ring = ctx.enter_context(tc.tile_pool(name="ring", bufs=1))
        psum = ctx.enter_context(tc.psum_pool(name="psum", bufs=1))
        ctx.enter_context(tc.manual_schedule())

        def kept(shape, dtype, name):
            return keep.tile(shape, dtype, name=name, align_bytes=64)

        def new_bank(shape, number, dtype=F32):
            return psum.tile(shape, dtype, name="bank%d" % number)

        def new_stage():
            tile = ring.tile([P, GROUP * PACK], BF16, name="stage", bufs=STAGE_BUFS, align_bytes=64)
            return tile[:]

        def new_x_or_rows(shape, dtype):
            return ring.tile(shape, dtype, name="x_or_rows", bufs=X_BUFS, align_bytes=64)

        def new_side(shape, dtype):
            return ring.tile(shape, dtype, name="side", bufs=1, align_bytes=64)

        def frame_rows(src, half):
            return src[HALF * half : HALF * (half + 1), :].rearrange("(a p) n -> p a n", p=P)

        def weight_rows(w, k, col):
            return w[GROUP * k : GROUP * (k + 1), col : col + GROUP].rearrange("(p j) c -> p j c", j=PACK)

        def source(key):
            name, first, second = key
            if name == "x":
                return frame_rows(x[:, first, :], second)
            if name == "dt":
                return frame_rows(dt, second)
            return weight_rows(wj if name == "wj" else wg, first, GROUP * second)

        load_order = [
            ("x", 0, 0), ("x", 0, 1), ("wj", 0, 0), ("wj", 1, 0), ("wj", 1, 1), ("wj", 0, 1),
            ("x", 1, 0), ("x", 1, 1), ("wg", 0, 0), ("dt", 0, 0), ("dt", 0, 1), ("wj", 2, 0), ("wj", 2, 1),
            ("wg", 1, 0), ("wj", 3, 0), ("wg", 0, 2), ("wj", 3, 1), ("wg", 1, 2), ("wg", 0, 1), ("wg", 1, 3),
            ("wg", 1, 1), ("wg", 0, 3),
        ]
        raw = {}

        def load_next(count):
            for key in load_order[len(raw) : len(raw) + count]:
                src = source(key)
                raw[key] = ring.tile(list(src.shape), BF16, name="raw", bufs=RAW_BUFS, align_bytes=64)
                nc.sync.dma_start(out=raw[key][:], in_=src)

        ident = kept([P, P], F32, "ident")
        make_identity(nc, ident[:])
        ident16 = kept([P, P], BF16, "ident16")
        make_identity(nc, ident16[:])

        d_raw = [kept([P, 2, 2 * GROUP], U8, "d_raw0"), new_side([P, 2, 2 * GROUP], U8)]
        d_raw_scales = kept([P, 2, PIX], U8, "d_raw_scales")
        nc.vector.memset(d_raw_scales[:].bitcast(I32), 0)
        factor_rows = kept([P, GROUP], BF16, "factor_rows")
        nc.vector.memset(factor_rows[:], 0.0)

        def load_d(g):
            src = d_words[:, :, 2 * GROUP * g : 2 * GROUP * (g + 1)].rearrange("k p n -> p k n")
            nc.sync.dma_start(out=d_raw[g][:].bitcast(I32), in_=src.bitcast(I32))

        load_d(0)
        for quad in range(4):
            nc.sync.dma_start(
                out=d_raw_scales[32 * quad : 32 * quad + 4, :, :].bitcast(I32),
                in_=d_scales[:, 4 * quad : 4 * quad + 4, :].rearrange("k r n -> r k n").bitcast(I32),
            )
        load_next(2)
        load_d(1)
        nc.sync.dma_start(out=factor_rows[0:UNIT_ROW, :], in_=h.rearrange("i (g n) -> (i g) n", g=2))
        load_next(1)
        nc.sync.dma_start(out=factor_rows[UNIT_ROW:DAMP_ROW, :], in_=unit.rearrange("i (g n) -> (i g) n", g=2))
        nc.sync.dma_start(out=factor_rows[DAMP_ROW:FACTOR_ROWS, :], in_=damp.rearrange("(g n) -> g n", g=2))
        load_next(RAW_BUFS - len(raw))

        d_codes = [kept([P, 2, PACK, 2 * P], U8, "d_codes%d" % g) for g in range(2)]
        d_planes = [kept([P, 2, PACK, P], U8, "d_planes%d" % g) for g in range(2)]

        def order_d_codes(g, ks):
            for k in ks:
                nc.vector.tensor_copy(
                    out=d_codes[g][:, k, :, :].rearrange("p t (mm m b) -> p mm t m b", m=8, b=2),
                    in_=d_raw[g][:, k, :].rearrange("p (mm m t b) -> p mm t m b", m=8, t=PACK, b=2),
                )

        def order_d_scales(g):
            nc.vector.tensor_copy(
                out=d_planes[g][:].rearrange("p k t (mm m) -> p k mm t m", m=16),
                in_=d_raw_scales[:, :, GROUP * g : GROUP * (g + 1)].rearrange(
                    "p k (mm m t) -> p k mm t m", m=16, t=PACK
                ),
            )

        x_grouped = {}

        def turn_x(i, half, numbers):
            words = raw["x", i, half][:].bitcast(F32)
            for g in range(2):
                if half == 0:
                    x_grouped[i, g] = new_x_or_rows([P, F * PACK], BF16)
                bank = new_bank([P, 2, HALF], numbers[g])
                for a in range(2):
                    for u in range(2):
                        nc.tensor.transpose(
                            bank[:, u, P * a : P * (a + 1)],
                            words[:, a, 2 * P * g + u : 2 * P * (g + 1) : 2],
                            ident[:],
                        )
                dst = x_grouped[i, g][:].bitcast(F32)[:, 2 * HALF * half : 2 * HALF * (half + 1)]
                nc.scalar.copy(
                    out=dst.rearrange("p (f u) -> p f u", u=2), in_=bank[:].rearrange("p u f -> p f u")
                )
            load_next(1)

        factors = new_bank([P, PACK, P], FACTOR_BANK, BF16)
        unit_damp = kept([P, PACK, FACTOR_ROWS - UNIT_ROW], F32, "unit_damp")
        h_unit = kept([P, PACK, UNIT_ROW], F32, "h_unit")

        def turn_factors():
            for t in ALL_SLOTS:
                nc.tensor.transpose(factors[:, t, :], factor_rows[:, t:GROUP:PACK], ident16[:])
            nc.scalar.copy(out=unit_damp[:], in_=factors[:, :, UNIT_ROW:FACTOR_ROWS])

        def damp_of(g, t):
            col = DAMP_ROW - UNIT_ROW + g
            return unit_damp[:, t, col : col + 1]

        def multiply_h_unit():
            nc.vector.tensor_tensor(
                out=h_unit[:], in0=factors[:, :, 0:UNIT_ROW], in1=unit_damp[:, :, 0:UNIT_ROW], op=MULT
            )

        dt_damped = [kept([P, PACK, F], F32, "dt_damped%d" % g) for g in range(2)]

        def turn_dt(g, numbers):
            for u in range(2):
                bank = new_bank([P, F], numbers[u])
                for a in range(F // P):
                    words = raw["dt", 0, a // 2][:].bitcast(F32)
                    nc.tensor.transpose(
                        bank[:, P * a : P * (a + 1)],
                        words[:, a % 2, 2 * P * g + u : 2 * P * (g + 1) : 2],
                        ident[:],
                    )
                pairs = bank[:].bitcast(BF16).rearrange("p (f e) -> p f e", e=2)
                for e in range(2):
                    t = 2 * u + e
                    nc.scalar.activation(
                        out=dt_damped[g][:, t, :], in_=pairs[:, :, e], func=COPY, scale=damp_of(g, t)
                    )

        codes, planes, grouped = {}, {}, {}

        def quantize(key, part=(0, PACK)):
            if key not in codes:
                label = "_".join([str(item) for item in key])
                codes[key] = kept([P, GROUP], U32, "codes_" + label)
                planes[key] = kept([P, GROUP], U8, "planes_" + label)
            cols = slice(P * part[0], P * part[1])
            nc.vector.quantize_mx(
                out=codes[key][:, cols].bitcast(FP8X4), scales=planes[key][:, cols], in_=grouped[key, part[0]]
            )

        def quantize_x(i):
            for g in range(2):
                grouped[("x", i, g), 0] = x_grouped[i, g][:]
                quantize(("x", i, g))

        def lay_on_scalar(key):
            grouped[key, 0] = new_stage()
            nc.scalar.copy(
                out=grouped[key, 0].rearrange("p (t mm m j) -> p mm t m j", t=PACK, m=2, j=PACK),
                in_=raw[key][:].rearrange("p j (mm m t) -> p mm t m j", m=2, t=PACK),
            )
            load_next(1)

        def gpsimd_copy(out, in_):
            nc.gpsimd.tensor_scalar(out=out, in0=in_, scalar1=1.0, scalar2=0.0, op0=MULT, op1=ADD)

        def lay_on_gpsimd(work):
            tile = new_side([P, SIDE_SLOTS * GROUP], BF16)
            col = 0
            for key, (t0, t1) in work:
                grouped[key, t0] = tile[:, col : col + (t1 - t0) * GROUP]
                gpsimd_copy(
                    grouped[key, t0].rearrange("p (t m j) -> p t m j", m=P, j=PACK),
                    raw[key][:].rearrange("p j (m t) -> p t m j", t=PACK)[:, t0:t1, :, :],
                )
                col = col + (t1 - t0) * GROUP
                if t1 == PACK:
                    load_next(1)

        def quantize_side(work):
            for key, part in work:
                quantize(key, part)

        low, high = [2, 3, 0, 1], [4, 5, 6, 7]
        bank_of = {
            (1, 0): [4, 5, 6, 0], (1, 1): [1, 2, 3, 4], (1, 2): [4, 5, 6, 2], (1, 3): [3, 0, 1, 4],
            (2, 0): low, (2, 1): high, (3, 0): low, (3, 2): high, (3, 1): high, (3, 3): high,
        }
        depth = {1: PIX // GROUP, 2: U * PIX // GROUP, 3: C // GROUP}
        banks = {}

        def passes(stage, out_group, ks, slots=ALL_SLOTS):
            for t in slots:
                if ks[0] == 0:
                    banks[stage, out_group, t] = new_bank([P, F], bank_of[stage, out_group][t])
                for k in ks:
                    if stage == 1:
                        i, g = divmod(out_group, 2)
                        lhs = d_codes[g][:, k, t, :].bitcast(FP4X4)
                        lhs_scale = d_planes[g][:, k, t, :]
                        moving = ("x", i, k)
                    else:
                        weight = ("wj" if stage == 2 else "wg", k, out_group)
                        lhs = codes[weight][:, P * t : P * (t + 1)].bitcast(FP8X4)
                        lhs_scale = planes[weight][:, P * t : P * (t + 1)]
                        moving = ("wbar" if stage == 2 else "r", k)
                    nc.tensor.matmul_mx(
                        out=banks[stage, out_group, t][:],
                        lhsT=lhs,
                        lhsT_scale=lhs_scale,
                        rhs=codes[moving][:].bitcast(FP8X4),
                        rhs_scale=planes[moving][:],
                        start=(k == 0),
                        stop=(k == depth[stage] - 1),
                    )

        flow = [kept([P, U, PACK, F], F32, "flow%d" % g) for g in range(2)]

        def add_x(n):
            i, g = divmod(n, 2)
            columns = x_grouped[i, g][:].rearrange("p (f t) -> p f t", t=PACK)
            for t in ALL_SLOTS:
                nc.vector.tensor_tensor(
                    out=flow[g][:, i, t, :], in0=banks[1, n, t][:], in1=columns[:, :, t], op=ADD
                )

        def scale_wbar(n):
            i, g = divmod(n, 2)
            grouped[("wbar", n), 0] = new_stage()
            nc.vector.tensor_tensor(
                out=grouped[("wbar", n), 0].rearrange("p (c e t) -> p c t e", e=2, t=PACK),
                in0=flow[g][:, i, :, :].rearrange("p t (c e) -> p c t e", e=2),
                in1=factors[:, :, n].unsqueeze(1).unsqueeze(3).to_broadcast([P, F // 2, PACK, 2]),
                op=MULT,
            )

        r_by_slot = {}

        def finish_r(g):
            r_by_slot[g] = new_stage()
            for t in ALL_SLOTS:
                nc.vector.scalar_tensor_tensor(
                    out=r_by_slot[g][:, F * t : F * (t + 1)],
                    in0=banks[2, g, t][:],
                    scalar=damp_of(g, t),
                    in1=dt_damped[g][:, t, :],
                    op0=MULT,
                    op1=ADD,
                )

        def group_r(g, copies):
            grouped[("r", g), 0] = new_stage()
            dst = grouped[("r", g), 0].rearrange("p (f t) -> p f t", t=PACK)
            src = r_by_slot[g].rearrange("p (t f) -> p f t", t=PACK)
            share = F // len(copies)
            for turn, copy in enumerate(copies):
                frames = slice(share * turn, share * (turn + 1))
                copy(out=dst[:, frames, :], in_=src[:, frames, :])

        def finish_y(n):
            i, g = divmod(n, 2)
            for t in ALL_SLOTS:
                nc.vector.scalar_tensor_tensor(
                    out=flow[g][:, i, t, :],
                    in0=flow[g][:, i, t, :],
                    scalar=h_unit[:, t, n : n + 1],
                    in1=banks[3, n, t][:],
                    op0=MULT,
                    op1=SUB,
                )

        def store_y(n, half):
            i, g = divmod(n, 2)
            rows = new_x_or_rows([P, 2, GROUP], F32)
            for a in range(2):
                bank = new_bank([P, PACK, P], low[2 * half + a])
                f0 = HALF * half + P * a
                for t in ALL_SLOTS:
                    nc.tensor.transpose(bank[:, t, :], flow[g][:, i, t, f0 : f0 + P], ident[:])
                nc.scalar.copy(
                    out=rows[:, a, :].rearrange("p (m t) -> p m t", t=PACK),
                    in_=bank[:].rearrange("p t m -> p m t"),
                )
            nc.sync.dma_start(out=frame_rows(out_0[:, i, GROUP * g : GROUP * (g + 1)], half), in_=rows[:])

        y_grouped = {}

        def round_y(g, half, copy, tile):
            y_grouped[g, half] = tile
            copy(
                out=tile.rearrange("p (c e s) -> p c s e", e=2, s=U * PACK),
                in_=flow[g][:, :, :, HALF * half : HALF * (half + 1)].rearrange("p i t (c e) -> p c (i t) e", e=2),
            )

        y_planes = [kept([P, F * U], U8, "y_planes%d" % g) for g in range(2)]

        def quantize_y(g, half):
            y_codes = kept([P, HALF * U], U32, "y_codes%d_%d" % (g, half))
            cols = slice(HALF * U * half, HALF * U * (half + 1))
            nc.vector.quantize_mx(
                out=y_codes[:].bitcast(FP8X4), scales=y_planes[g][:, cols], in_=y_grouped[g, half]
            )
            nc.sync.dma_start(
                out=out_1[g].rearrange("p m t -> p (m t)").bitcast(I32)[:, cols], in_=y_codes[:].bitcast(I32)
            )

        def store_y_planes(g):
            for quad in range(4):
                nc.sync.dma_start(
                    out=out_2[g, 4 * quad : 4 * quad + 4, :].bitcast(I32),
                    in_=y_planes[g][32 * quad : 32 * quad + 4, :].bitcast(I32),
                )

        on_scalar = nc.scalar.copy
        on_vector = nc.vector.tensor_copy

        whole, front, back = (0, PACK), (0, 2), (2, PACK)
        side_work = [
            [(("wj", 1, 0), whole), (("wj", 1, 1), whole), (("wg", 0, 0), front)],
            [(("wg", 0, 0), back), (("wg", 1, 0), whole), (("wg", 0, 2), whole)],
            [(("wg", 1, 3), whole)],
        ]

        order_d_codes(0, [0, 1])
        turn_x(0, 0, [0, 1])
        order_d_scales(0)
        turn_x(0, 1, [2, 3])
        turn_factors()
        order_d_scales(1)
        order_d_codes(1, [0])
        quantize_x(0)
        passes(1, 0, [0])
        passes(1, 0, [1])
        order_d_codes(1, [1])

        lay_on_scalar(("wj", 0, 0))
        lay_on_gpsimd(side_work[0])
        lay_on_scalar(("wj", 0, 1))
        passes(1, 1, [0, 1], [0, 1, 2])
        add_x(0)
        passes(1, 1, [0, 1], [3])
        turn_x(1, 0, [5, 6])
        add_x(1)
        turn_x(1, 1, [0, 1])
        turn_dt(0, low[0:2])
        turn_dt(1, low[2:4])
        load_next(2)
        scale_wbar(0)
        scale_wbar(1)
        multiply_h_unit()

        quantize_x(1)
        passes(1, 2, [0, 1])
        passes(1, 3, [0, 1], [0, 1, 2])
        for key in [("wj", 0, 0), ("wj", 0, 1), ("wbar", 0), ("wbar", 1)]:
            quantize(key)
        for key in [("wj", 2, 0), ("wj", 2, 1), ("wj", 3, 0), ("wj", 3, 1)]:
            lay_on_scalar(key)
        quantize_side(side_work[0])

        lay_on_gpsimd(side_work[1])
        add_x(2)
        passes(1, 3, [0, 1], [3])
        add_x(3)
        passes(2, 0, [0, 1])
        passes(2, 1, [0, 1], [0, 1, 2])
        scale_wbar(2)
        scale_wbar(3)
        passes(2, 1, [0, 1], [3])

        quantize(("wj", 2, 0))
        quantize(("wbar", 2))
        passes(2, 0, [2])
        lay_on_scalar(("wg", 1, 2))
        lay_on_scalar(("wg", 0, 1))
        quantize(("wj", 3, 0))
        quantize(("wbar", 3))
        passes(2, 0, [3])
        quantize(("wj", 2, 1))
        quantize(("wj", 3, 1))
        passes(2, 1, [2, 3])
        quantize_side(side_work[1])

        lay_on_gpsimd(side_work[2])
        finish_r(0)
        group_r(0, [on_scalar])
        finish_r(1)
        group_r(1, [on_scalar, on_vector])
        lay_on_scalar(("wg", 1, 1))
        lay_on_scalar(("wg", 0, 3))
        quantize(("r", 0))
        passes(3, 0, [0])
        quantize(("wg", 1, 2))
        quantize(("r", 1))
        passes(3, 0, [1])
        passes(3, 2, [0, 1])
        quantize(("wg", 0, 1))

        finish_y(0)
        store_y(0, 0)
        store_y(0, 1)
        quantize(("wg", 1, 1))
        finish_y(2)
        quantize(("wg", 0, 3))
        round_y(0, 0, on_vector, new_stage())
        quantize_side(side_work[2])

        side_tile = new_side([P, PACK * GROUP], BF16)
        round_y(0, 1, gpsimd_copy, side_tile[:])
        for n, done in [(1, 2), (3, 1)]:
            passes(3, n, [0, 1], [0, 1, 2])
            store_y(done, 0)
            passes(3, n, [0, 1], [3])
            store_y(done, 1)
            finish_y(n)

        quantize_y(0, 0)
        round_y(1, 0, on_vector, new_stage())
        quantize_y(0, 1)
        store_y_planes(0)
        store_y(3, 0)
        round_y(1, 1, on_vector, new_stage())
        store_y(3, 1)
        quantize_y(1, 0)
        quantize_y(1, 1)
        store_y_planes(1)
